import numpy as np, ml_dtypes
CORES = [2,7,18,23,34]
N = 5
BF = ml_dtypes.bfloat16
W, L, S, J, TB, D = 4096, 256, 16, 32, 2, 3
NE = (TB + 1) // 2 * L
def cands(u, k):
    return ((u * u >> 5)[..., None] + (2 * np.arange(J) + 1) * u[..., None] + k) & (W - 1)
def pairs(rng, n, pen):
    s = np.arange(W) % S
    kv = rng.random(W) + pen * ((s < TB) & (s % 2 == 0)); ky = rng.random(W) + pen * ((s < TB) & (s % 2 == 1))
    row = np.full(W, -1, np.int64); row[rng.permutation(np.argsort(kv)[:n])] = np.argsort(ky)[:n]
    return row
def filled(rng, lo, hi):
    return np.stack([np.stack([pairs(rng, int(W * (lo + (hi - lo) * rng.random())), 0.6) for g in range(8)]) for r in range(N)])
def pack(x, a, w):
    b = np.full((N, 8, W), -1, np.int64)
    for r in range(N):
        for g in range(8):
            v = np.flatnonzero(a[r, g] >= 0); b[(r + 1) % N, g, a[r, g, v]] = v
    return {"x": np.ascontiguousarray(x).reshape(N, 128, W).astype(np.float32).astype(BF), "pa": a.astype(np.int32), "pb": b.astype(np.int32), "wt": np.ascontiguousarray(w).reshape(N, 128, 1).astype(np.int32)}
def some(rng, m):
    us = np.flatnonzero(m)
    return int(us[int(rng.integers(0, us.size))]) if us.size else 0
def hashed(z, w, u):
    z = np.array(z); z[:2] = 0; rho = (u - int(np.sum(w * z))) & (W - 1); z[0] = rho & 255; z[1] = rho >> 8
    return z
def firststep(x, a, w, r):
    q = (r + 1) % N; v = S * np.arange(L); z = x[r][:, :, v]; u = np.sum(w[q][:, :, None] * z, axis=1) & (W - 1); c = cands(u, 0)
    col = np.take_along_axis(x[q], c.reshape(8, 1, L * J), 2).reshape(8, 16, L, J); key = np.sum(np.abs(col - z[..., None]), axis=1) * W + c
    y = np.take_along_axis(c, np.argmin(key, axis=2)[..., None], 2)[..., 0]; taken = np.zeros((8, W), bool)
    for g in range(8): taken[g, a[r, g][a[r, g] >= 0]] = True
    return y, (a[r][:, v] < 0) & ~np.take_along_axis(taken, y, 1), taken
def setup_inputs(rng):
    return pack(rng.integers(0, 256, (N, 8, 16, W)), filled(rng, 0.4, 0.85), rng.integers(1, 4096, (N, 8, 16)))
def setup_inputs_spread(rng):
    x = np.minimum(np.exp2(8 * rng.random((N, 8, 1, W))) * rng.random((N, 8, 16, W)) * 1.25, 255).astype(np.int64) * (rng.random((N, 8, 1, W)) > 0.0625)
    w = np.minimum(np.maximum(np.exp2(12 * rng.random((N, 8, 16))).astype(np.int64), 1), 4095)
    return pack(x, filled(rng, 0.05, 0.95), w)
def setup_inputs_ties(rng):
    recs = rng.integers(0, 256, (1, 8, 16, 12)); recs[..., 0] = 0; recs[..., 1] = 0; recs[:, :, 0, 1] = 1
    pick = rng.integers(0, 12, (N, 8, W)); w = rng.integers(1, 4096, (N, 8, 16)); w[:, :, 0] = 2048
    x = np.take_along_axis(np.ascontiguousarray(np.broadcast_to(recs, (N, 8, 16, 12))), pick[:, :, None, :], 3)
    return pack(x, filled(rng, 0.3, 0.9), w)
def setup_inputs_corners(rng):
    x = rng.integers(0, 256, (N, 8, 16, W)); col = rng.random((N, 8, 1, W)); x = np.where(col < 0.06, 0, np.where(col > 0.94, 255, x))
    w = rng.integers(1, 4096, (N, 8, 16)); k = rng.integers(0, 4, (N, 8, 1)); w = np.where(k == 0, 1, np.where(k == 1, 4095, w))
    off = int(rng.integers(0, 8)); a = np.full((N, 8, W), -1, np.int64); s = np.arange(W)
    for r in range(N):
        for g in range(8):
            m = (r + g + off) % 8
            if m == 1: a[r, g] = rng.permutation(W)
            elif m == 2: a[r, g] = pairs(rng, W - NE, 2.0)
            elif m == 3: a[r, g, np.delete(s, W - S)] = rng.permutation(W - 1)
            elif m == 4 or m == 5:
                v = np.flatnonzero(pairs(rng, W // 2 if m == 4 else 3 * W // 4, 0.6) >= 0); a[r, g, v] = v if m == 4 else W - 1 - v
            elif m == 6:
                a[r, g] = pairs(rng, 3 * W // 4, 2.0); rec = rng.integers(0, 256, (16, 1))
                for t in range(0, TB, 2): x[r, g][:, t::S] = rec
    tab = cands(np.arange(W), 0); starter = (s % S < TB) & (s % S % 2 == 0)
    for r in range(N):
        g = (7 - r - off) % 8; q = (r + 1) % N; w[q, g, 0] = 1; w[q, g, 1] = 256
        lanes = np.concatenate([np.arange(0, 32, 2 - r % 2), np.arange(32, 96)]); pl = np.where(lanes < 32, 97 + lanes, 128 + lanes)
        held = a[r - 1, g]; held = held[held >= 0]; held = held[held % S >= TB]; h = rng.permutation(held)[:lanes.size]
        row = np.full(W, -1, np.int64); row[h] = pl[:h.size]; fv = ~starter; fv[h] = False; fy = np.ones(W, bool); fy[96:129] = False; fy[160:224] = False
        row[rng.permutation(np.flatnonzero(fv))[:W // 2]] = rng.permutation(np.flatnonzero(fy))[:W // 2]; a[r, g] = row
        for e in range(h.size):
            k = int(lanes[e]); P = int(pl[e]); z = hashed(rng.integers(0, 256, 16), w[q, g], some(rng, np.any(tab == P, axis=1)))
            if k < 32: there = z; back = np.zeros(16, np.int64)
            else:
                kk = (k - 32) >> 1 if r % 2 == 1 else 2 * ((k - 32) >> 2)
                hit = ((tab + 97 + kk) & (W - 1)) == P; there = hashed(z, w[q, g], some(rng, np.any(hit, axis=1) & ~np.all(hit, axis=1))); back = there
            x[r, g][:, S * k] = z; x[q, g][:, P] = there; x[r, g][:, int(h[e])] = back
    for r in range(0, N, 2):
        g = (7 - r - off) % 8; y, go, taken = firststep(x, a, w, r); n = 0
        for b in range(8): n = n + int(np.unique(y[b][go[b]]).size)
        if n % 2 == 1:
            cnt = np.bincount(y[g][go[g]], minlength=W); one = np.flatnonzero(go[g] & (cnt[y[g]] == 1) & (np.arange(L) >= 96))
            fr = ~taken[g]; fr[y[g]] = False; fr[96:129] = False; fr[160:224] = False; fr = np.flatnonzero(fr)
            if one.size and fr.size: a[r, g, S * int(one[int(rng.integers(0, one.size))])] = int(fr[int(rng.integers(0, fr.size))])
    return pack(x, a, w)
def setup_inputs_ends(rng):
    kind = (7 - np.arange(8)[None, :] + N - 1 - np.arange(N)[:, None]) % 4
    w = np.where(rng.random((N, 8, 16)) < 0.5, 1, 4095); w[kind == 0] = 4095; w[kind == 3] = 1
    x = 255 * (rng.random((N, 8, 16, W)) < rng.choice(np.array([0.0, 0.25, 0.5, 0.75, 1.0]), (N, 8, 1, W))).astype(np.int64)
    pick = rng.random((N, 8, L)) < 0.25; pick[:, :, L - 1] = True; x[:, :, :, ::S] = np.where(pick[:, :, None, :], 255, x[:, :, :, ::S])
    tab = cands(np.arange(W), 0); top = np.max(tab, axis=1); pool = np.flatnonzero(top == np.max(top))
    a = np.full((N, 8, W), -1, np.int64); n = 3 * W // 8
    for r in range(N):
        for g in range(8):
            if kind[r, g] == 1:
                need = int(pool[int(rng.integers(0, pool.size))]) * 3839; i = int(rng.integers(0, 16)); o = (i + 1) % 16; w[r, g, i] = 0
                if (need - int(np.sum(w[r, g]))) & (W - 1) == 0: w[r, g, o] = 4096 - w[r, g, o]
                w[r, g, i] = (need - int(np.sum(w[r, g]))) & (W - 1)
            c = cands(np.array([255 * int(np.sum(w[r, g])) & (W - 1)]), 0)[0]; c = c[c % S != 0]
            if c.size:
                x[r, g][:, c] = 0
                if kind[r, g] == 2: x[r, g][:, int(np.max(c))] = 255
            v = rng.permutation(W); v = v[(v != 0) & (v != W - 1) & (v != W - S)][:n]; y = rng.permutation(W); y = y[(y != 0) & (y != W - 1)][:n]
            a[r, g, v] = y
            if g % 2 == 0: a[r, g, 0] = W - 1; a[r, g, W - 1] = 0
    return pack(x, a, w)
def setup_inputs_paths(rng):
    x = rng.integers(0, 256, (N, 8, 16, W)); w = rng.integers(1, 4096, (N, 8, 16)); w[:, :, 0] = 1; w[:, :, 1] = 256
    tab = cands(np.arange(W), 0); s = np.arange(W); gs = rng.permutation(8); lanes = np.argsort(rng.random((N, 8, L)), axis=-1); cnt = np.zeros((N, 8), np.int64)
    use = np.zeros((N, 8, W), bool); use[:, :, s % S < TB] = True; use[:, :, 1850:1920] = True; use[:, :, 3770:3840] = True
    for o in range(0, W, 1024): use[:, :, o + 96:o + 256] = True
    fv = [[[] for g in range(8)] for r in range(N)]; fy = [[[] for g in range(8)] for r in range(N)]; link = [[[] for g in range(8)] for r in range(N)]
    k0 = np.zeros(N, np.int64); k1 = np.zeros(N, np.int64)
    def start(r, g):
        v = S * int(lanes[r, g, cnt[r, g]]); cnt[r, g] += 1; fv[r][g].append(v)
        return v
    def spot(r, g):
        c = np.flatnonzero(~use[r, g]); p = int(c[int(rng.integers(0, c.size))]); use[r, g, p] = True
        return p
    def reach(r, g, k, v=None, u=0):
        z = rng.integers(0, 256, 16)
        for e in range(40):
            z = rng.integers(0, 256, 16)
            if v is not None: z = hashed(z, v, u)
            c = cands(np.array([int(np.sum(w[r, g] * z)) & (W - 1)]), k)[0]; c = c[~use[r, g, c]]
            if c.size:
                p = int(c[int(rng.integers(0, c.size))]); use[r, g, p] = True
                return z, p
        return z, -1
    def visit(r, g, P, rec, b):
        q = (r + 1) % N; m = np.any(tab == P, axis=1)
        if not np.any(m): return None
        z = hashed(rng.integers(0, 256, 16), w[q, g], some(rng, m)); v = start(r, g)
        if b < 0: b = spot(r, g)
        x[r, g][:, v] = z; x[q, g][:, P] = z; x[r, g][:, b] = rec; link[r][g].append((b, P))
        return z
    for r in range(N):
        q = (r + 1) % N; g = int(gs[0])
        for i in range(L):
            z, p = reach(q, g, 0)
            if p >= 0: x[r, g][:, S * i] = z; x[q, g][:, p] = z; fv[r][g].append(S * i); fy[r][g].append(p); k0[q] += 1
        g = int(gs[1]); xq = x[q, g]
        z = hashed(rng.integers(200, 256, 16), w[q, g], 4095); x[r, g][:, start(r, g)] = z; c = cands(np.array([4095]), 0)[0]
        j = 2 * int(rng.integers(1, J // 2)); xq[:, c] = 0; xq[5, c[j]] = 8; xq[5, c[j - 1]] = 8; fy[r][g].append(int(c[j])); fy[r][g].append(int(c[j - 1]))
        z = hashed(rng.integers(200, 256, 16), w[q, g], 2047); x[r, g][:, start(r, g)] = z; c = cands(np.array([2047]), 0)[0]
        xq[:, c] = 0; xq[6, c] = (int(np.sum(z)) - 4) & 15; xq[5, c[0]] = 1; fy[r][g].append(int(c[0])); k0[q] += 2
    ka = [int(k) & 31 for k in k0]
    for r in range(N):
        q = (r + 1) % N; g = int(gs[2])
        if q % 2 == 1:
            w[q, g, 2] = 0; need = (1024 + 2048 * int(rng.integers(0, 2))) * 3839
            if (need - int(np.sum(w[q, g]))) & (W - 1) == 0: w[q, g, 3] += 1 if w[q, g, 3] < 4095 else -1
            w[q, g, 2] = (need - int(np.sum(w[q, g]))) & (W - 1)
            if visit(r, g, 1024 + 97 + ka[q], np.full(16, 255, np.int64), -1) is not None:
                x[q, g][:, 3072 + 97 + ka[q]] = 0; fy[r][g].append(3072 + 97 + ka[q]); k1[q] += 1
        g = int(gs[4])
        if r % 2 == 1:
            for o in (0, 2048):
                rb, b = reach(r, g, 97 + ka[r], w[q, g], o); z, p = reach(r, g, 0)
                if b >= 0 and p >= 0 and visit(r, g, o + 97 + ka[q], rb, b) is not None:
                    fy[r][g].append(o + 194); v = start(r - 1, g); e = spot(r - 1, g)
                    x[r - 1, g][:, v] = z; x[r, g][:, p] = z; x[r - 1, g][:, e] = rb; link[r - 1][g].append((e, p)); fy[r - 1][g].append(b); k1[r] += 1
    kb = [int(k) & 31 for k in k1]
    for r in range(N):
        q = (r + 1) % N; g = int(gs[3])
        for o in (0, 2048):
            if visit(r, g, o + 97 + ka[q], hashed(rng.integers(0, 256, 16), w[q, g], o), -1) is not None: fy[r][g].append(o + 194 + kb[q])
        g = int(gs[5]); z1, p = reach(q, g, 97 + ka[q])
        if p >= 0:
            z = visit(r, g, 1024 + 194 + kb[q], z1, -1)
            if z is not None:
                z = hashed(z, w[q, g], 1024); b = spot(r, g); x[q, g][:, p] = z1; x[r, g][:, b] = z; link[r][g].append((b, p))
                x[q, g][:, 3072 + 194 + kb[q]] = np.where(z < 128, 255, 0); fy[r][g].append(3072 + 194 + kb[q])
    a = np.full((N, 8, W), -1, np.int64)
    for r in range(N):
        for g in range(8):
            mv = np.ones(W, bool); my = np.ones(W, bool); mv[np.array(fv[r][g], np.int64)] = False; my[np.array(fy[r][g], np.int64)] = False
            for v, y in link[r][g]: mv[v] = False; my[y] = False; a[r, g, v] = y
            vs = np.flatnonzero(mv); vs = np.concatenate([vs[vs % S == 0], rng.permutation(vs[vs % S != 0])[:W // 2]])
            a[r, g, vs] = rng.permutation(np.flatnonzero(my))[:vs.size]
    return pack(x, a, w)
def check_inputs(d):
    bad = []; xx = np.asarray(d["x"]).astype(np.float32)
    if not (np.min(xx) >= 0 and np.max(xx) <= 255): bad.append("range of x")
    if np.any(xx != np.floor(xx)): bad.append("x not whole")
    for k, lo, hi in (("pa", -1, W - 1), ("pb", -1, W - 1), ("wt", 1, 4095)):
        if not (np.min(d[k]) >= lo and np.max(d[k]) <= hi): bad.append("range of " + k)
    own = np.arange(W)[None, :]; off = False
    for r in range(N):
        a = np.asarray(d["pa"])[r].astype(np.int64); b = np.asarray(d["pb"])[(r + 1) % N].astype(np.int64)
        for c, e in ((a, b), (b, a)):
            if np.any((c >= 0) & (np.take_along_axis(e, np.clip(c, 0, W - 1), 1) != own)): off = True
    if off: bad.append("pa and pb not mutual")
    return bad
def reference(x, pa, pb, wt):
    X = x.astype(np.float32).astype(np.int32).reshape(N, 8, 16, W); A = pa.astype(np.int64); B = pb.astype(np.int64); w = wt.astype(np.int64).reshape(N, 8, 16, 1)
    kap = np.zeros(N, np.int64); lane = np.arange(L)
    for t in range(TB):
        q = (np.arange(N) + (1 if t % 2 == 0 else -1)) % N
        near, far = (A, B) if t % 2 == 0 else (B, A)
        v = S * lane + t; x0 = X[:, :, :, v]; z = x0; live = near[:, :, v] < 0; last = np.full((N, 8, L), -1, np.int64)
        for d in range(D):
            u = np.sum(w[q] * z, axis=2) & (W - 1)
            c = cands(u, (97 * d + kap[q])[:, None, None, None])
            col = np.take_along_axis(X[q], c.reshape(N, 8, 1, L * J), 3).reshape(N, 8, 16, L, J)
            dist = np.sum(np.abs(col - z[..., None]), axis=2)
            key = np.where(c == last[..., None], 2 ** 24, dist.astype(np.int64) * W + c)
            y = np.take_along_axis(c, np.argmin(key, axis=3)[..., None], 3)[..., 0]
            go = live & (np.take_along_axis(far[q], y, 2) < 0)
            rr, gg, ii = np.nonzero(go); low = np.full((N, 8, W), L, np.int64); np.minimum.at(low, (rr, gg, y[go]), ii)
            win = go & (np.take_along_axis(low, y, 2) == lane)
            rr, gg, ii = np.nonzero(win); yy = y[win]; qq = q[rr]; vv = S * ii + t
            X[qq, gg, :, yy] = (X[qq, gg, :, yy] + x0[rr, gg, :, ii]) >> 1
            far[qq, gg, yy] = vv; near[rr, gg, vv] = yy
            live = live & ~win; kap = np.bincount(qq, minlength=N).astype(np.int64) & 31; last = y
            p = np.maximum(np.take_along_axis(far[q], y, 2), 0)
            z = np.where(live[:, :, None, :], np.take_along_axis(X, p[:, :, None, :], 3), z)
    return {"yx": X.reshape(N, 128, W).astype(np.float32).astype(BF), "ya": A.astype(np.float32), "yb": B.astype(np.float32)}

@@ -1,0 +1,424 @@
+from concourse.mybir import AluOpType as OP, AxisListType, ActivationFunctionType as AF
+
+N = 5
+WN = 4096
+WD = 4352
+STEPS = 3
+CH = [("S", 0, 4), ("S", 4, 8), ("R", 28, 32), ("S", 8, 12), ("S", 12, 16), ("S", 16, 20), ("S", 20, 24), ("S", 24, 26), ("S", 26, 28)]
+SPLIT = 28
+
+SCRATCH = {}
+for _n, _c, _d in (
+        ("X", WD, "bfloat16"), ("XR0", WD, "bfloat16"), ("XR1", WD, "bfloat16"), ("OA", WD, "float32"), ("OB", WD, "float32"),
+        ("IOTA", WD + 8, "float32"), ("A", 8192, "bfloat16"), ("M", 8192, "bfloat16"), ("zb", 256, "bfloat16"),
+        ("pai", 256, "int32"), ("pbi", 256, "int32"), ("wti", 1, "int32"), ("wf", 1, "float32"), ("wg", 1, "float32"),
+        ("pidx", 1, "int32"), ("pmi", 1, "int32"), ("pgi", 1, "int32"), ("pidf", 1, "float32"), ("pmf", 1, "float32"), ("pgf", 1, "float32"), ("pg15", 1, "float32"),
+        ("a0", 1, "float32"), ("a1", 1, "float32"), ("a1n", 1, "float32"), ("q32", 1, "float32"), ("q32n", 1, "float32"), ("q33n", 1, "float32"), ("qsn", 1, "float32"),
+        ("col", 256, "float32"), ("colL", 512, "float32"), ("colJ", 512, "float32"), ("colg", 128, "float32"), ("dl", 512, "float32"), ("tj", 512, "float32"),
+        ("E1", 144, "bfloat16"), ("E8", 144, "bfloat16"), ("E4n", 144, "bfloat16"), ("EW", 144, "float16"),
+        ("I16", 128, "float16"), ("IB", 128, "bfloat16"), ("IBAR", 128, "bfloat16"), ("BO", 128, "bfloat16"), ("TRI", 128, "bfloat16"), ("ONES", 128, "bfloat16"),
+        ("DM", 256, "float32"), ("DMD", 256, "float32"), ("OFFB", 256, "bfloat16"), ("SEG", 256, "float32"), ("SEGB", 256, "float32"),
+        ("RC", 512, "float16"), ("RL", 512, "float16"), ("RO", 512, "float16"), ("vr0", 256, "float32"), ("vr1", 256, "float32"), ("DC", 16, "float32"),
+        ("ui", 16, "int32"), ("u", 16, "int32"), ("sq", 16, "int32"), ("hm", 16, "int32"), ("TA", 34, "float16"), ("TB", 34, "float16"), ("TAT", 128, "float16"), ("TBT", 128, "float16"),
+        ("CI", 512, "int32"), ("CM", 512, "int32"), ("LST", 512, "uint16"), ("c16", 512, "float16"), ("bar", 512, "bfloat16"),
+        ("ym", 16, "float32"), ("yi", 16, "int32"), ("y", 16, "int32"), ("yc", 16, "float32"), ("yl", 16, "uint16"), ("Yr", 256, "uint16"), ("Or", 256, "bfloat16"),
+        ("XG", 256, "bfloat16"), ("sm", 256, "float16"), ("t2", 256, "float32"), ("EQ", 2176, "bfloat16"), ("qs", 256, "float32"), ("nw", 16, "float32"), ("yw", 16, "float32"),
+        ("lf", 16, "float32"), ("pm", 256, "float32"), ("ps", 256, "float32"), ("pl16", 16, "uint16"), ("PLf", 16, "float32"), ("wb", 16, "bfloat16"), ("wd", 16, "float32"),
+        ("kf", 1, "float32"), ("ki", 1, "int32"), ("ka", 1, "int32")):
+    SCRATCH[_n] = ("sbuf", [128, _c], _d)
+for _t in range(2):
+    for _n, _c, _d in (("SS", 256, "bfloat16"), ("SR", 256, "bfloat16"), ("DS", 16, "float32"), ("DR", 16, "float32"), ("PS", 16, "uint16"), ("PR", 16, "uint16")):
+        SCRATCH["%s%d" % (_n, _t)] = ("sbuf", [128, _c], _d)
+    for _s in range(STEPS):
+        SCRATCH["XN%d" % _s] = ("sbuf", [128, 256], "bfloat16")
+        SCRATCH["L2%d" % _s] = ("sbuf", [128, 16], "uint16")
+        if _s < STEPS - 1:
+            SCRATCH["XI%d%d" % (_t, _s)] = ("sbuf", [128, 256], "bfloat16")
+            SCRATCH["LI%d%d" % (_t, _s)] = ("sbuf", [128, 16], "uint16")
+SCRATCH["oad"] = ("dram", [8, WN], "float32")
+SCRATCH["obd"] = ("dram", [8, WN], "float32")
+for _n, _c in (("pz", 1024), ("ph", 512), ("pt", 512), ("pc", 512), ("pla", 512), ("pk", 512), ("pq", 512)):
+    SCRATCH[_n] = ("psum", [128, _c], "float32")
+PARTS = ("ym", "RO", "TA", "A2")
+PSUM = ("pz", "ph", "pt", "pc", "pla", "pk", "pq")
+
+MSG = []
+for _t in range(2):
+    MSG += ["S%d" % _t, "B%d" % _t, "D%d" % _t, "P%d" % _t]
+    for _s in range(STEPS - 1):
+        MSG += ["X%d%d" % (_t, _s), "L%d%d" % (_t, _s)]
+SEMAPHORES = ["cv", "cs", "cp", "cg", "ldx", "ldw", "lda", "ldb", "sta", "stb", "roa", "rob", "outx", "outa", "outb"]
+SEMAPHORES += ["a" + m for m in MSG] + ["d" + m for m in MSG]
+
+
+def rank_program(g, core, T, topo):
+    me = T.rank_of(core)
+    if me is None:
+        return
+    queues = {"v": g.vector, "s": g.scalar, "p": g.tensor, "g": g, "y": g.sync}
+    csem = {"v": "cv", "s": "cs", "p": "cp", "g": "cg"}
+    count, waited, wr, rd = {}, {q: {} for q in queues}, {}, {}
+
+    def wait(q, toks):
+        for _, sem, val in toks:
+            if waited[q].get(sem, 0) < val:
+                waited[q][sem] = val
+                queues[q].wait_ge(T.sem[sem], val)
+
+    def before(q, reads, writes):
+        toks = []
+        for x in reads:
+            toks += wr.get(x, [])
+            if x in PSUM:
+                toks += [k for k in rd.get(x, []) if k[0] != q]
+        for x in writes:
+            toks += [k for k in wr.get(x, []) if k[0] != q or (q != "p" and x not in PARTS)]
+            toks += [k for k in rd.get(x, []) if k[0] != q]
+        best = {}
+        for k in toks:
+            if k[1] not in best or best[k[1]][2] < k[2]:
+                best[k[1]] = k
+        wait(q, best.values())
+
+    def after(tok, reads, writes):
+        for x in reads:
+            if x not in writes:
+                rd.setdefault(x, [])
+                rd[x] = [k for k in rd[x] if k[1] != tok[1]] + [tok]
+        for x in writes:
+            wr[x] = [tok]
+            rd[x] = []
+
+    def op(q, fn, reads, writes, **kw):
+        before(q, reads, writes)
+        sem = csem[q]
+        fn(**kw).then_inc(T.sem[sem], 1)
+        count[sem] = count.get(sem, 0) + 1
+        after((q, sem, count[sem]), reads, writes)
+
+    def dma(q, sem, pairs, reads, writes):
+        before(q, reads, writes)
+        for out, in_ in pairs:
+            queues[q].dma_start(out, in_).then_inc(T.sem[sem], 16)
+            count[sem] = count.get(sem, 0) + 16
+        after(("dma" + sem, sem, count[sem]), reads, writes)
+
+    def send(msg, dst, out, in_, reads):
+        before("g", reads, [])
+        eng = topo.engines(core, dst)[:8]
+        rid, pid, _ = topo.addr(dst)
+        g.remote_dma(out, in_, T.sem["a" + msg], T.sem["d" + msg], pid, rid, sum(1 << e for e in eng))
+        count["d" + msg] = len(eng)
+        after(("rdma" + msg, "d" + msg, len(eng)), reads, [])
+
+    def arrives(msg, src, buf):
+        n = len(topo.engines(src, core)[:8])
+        count["a" + msg] = n
+        after(("arr" + msg, "a" + msg, n), [], [buf])
+
+    def ts(out, w, in0, r, s1, op0, s2=None, op1=None, cols=()):
+        kw = {"out": out, "in0": in0, "scalar1": s1, "scalar2": s2, "op0": op0}
+        if op1 is not None:
+            kw["op1"] = op1
+        op("v", g.vector.tensor_scalar, list(r) + list(cols), w, **kw)
+
+    def tt(out, w, in0, in1, r, o):
+        op("v", g.vector.tensor_tensor, r, w, out=out, in0=in0, in1=in1, op=o)
+
+    def cp(out, w, in_, r):
+        op("v", g.vector.tensor_copy, r, w, out=out, in_=in_)
+
+    def mm(out, w, lhsT, rhs, r, start, stop):
+        op("p", g.tensor.matmul, r, w, out=out, lhsT=lhsT, rhs=rhs, start=start, stop=stop)
+
+    def act(out, w, in_, r, func, **kw):
+        op("s", g.scalar.activation, r, w, out=out, in_=in_, func=func, **kw)
+
+    def scan(out, w, d0, d1, r, init, o0, o1):
+        op("v", g.vector.tensor_tensor_scan, r, w, out=out, data0=d0, data1=d1, initial=init, op0=o0, op1=o1)
+
+    up, down = T.cores[(me + 1) % N], T.cores[(me - 1) % N]
+
+    dma("y", "ldx", [(T.X[:, 0:WN], T.x[:])], [], ["X"])
+    dma("y", "ldw", [(T.wti[:], T.wt[:])], [], ["wti"])
+    dma("y", "lda", [(T.pai[:], T.pa[:])], [], ["pai"])
+    dma("y", "ldb", [(T.pbi[:], T.pb[:])], [], ["pbi"])
+
+    def iota(name, pattern, base, mult, n):
+        kw = {"out": T[name][:, 0:n], "pattern": pattern, "base": base, "channel_multiplier": mult}
+        if name != "pidx":
+            kw["allow_small_or_imprecise_dtypes"] = True
+        op("g", g.iota, [], [name], **kw)
+
+    iota("pidx", [[0, 1]], 0, 1, 1)
+    iota("col", [[1, 256]], 0, 0, 256)
+    iota("colL", [[0, 32], [1, 16]], 0, 0, 512)
+    iota("colg", [[1, 8], [0, 16]], 0, 0, 128)
+    iota("colJ", [[2, 32], [0, 16]], 1, 0, 512)
+
+    def send_starts(t, dst):
+        act(T["SS%d" % t][:], ["SS%d" % t], T.X[:, t:WN:16], ["X"], AF.Copy)
+        send("S%d" % t, dst, T["SR%d" % t][:], T["SS%d" % t][:], ["SS%d" % t])
+        send("B%d" % t, dst, T["XR%d" % t][:, 0:WN], T.X[:, 0:WN], ["X"])
+
+    send_starts(0, up)
+    arrives("S0", down, "SR0")
+    arrives("B0", down, "XR0")
+    iota("IOTA", [[1, WD]], 0, 0, WD)
+
+    def fill(ap, w, c):
+        before("v", [], [w])
+        g.vector.memset(ap, c).then_inc(T.sem.cv, 1)
+        count["cv"] = count.get("cv", 0) + 1
+        after(("v", "cv", count["cv"]), [], [w])
+
+    fill(T.X[:, WN:WD], "Xd", 0.0)
+    fill(T.OA[:, WN:WD], "OAd", 0.0)
+    fill(T.OB[:, WN:WD], "OBd", 0.0)
+    fill(T.IOTA[:, WD:WD + 8], "IOTAd", -1.0)
+    fill(T.ONES[:], "ONES", 1.0)
+    fill(T.PLf[:], "PLf", 8192.0)
+    ts(T.pmi[:], ["pmi"], T.pidx[:], ["pidx"], 15, OP.bitwise_and)
+    ts(T.pgi[:], ["pgi"], T.pidx[:], ["pidx"], 4, OP.arith_shift_right)
+    cp(T.pidf[:], ["pidf"], T.pidx[:], ["pidx"])
+    cp(T.pmf[:], ["pmf"], T.pmi[:], ["pmi"])
+    cp(T.pgf[:], ["pgf"], T.pgi[:], ["pgi"])
+    ts(T.pg15[:], ["pg15"], T.pgf[:], ["pgf"], 16.0, OP.mult, 15.0, OP.add)
+    cp(T.wf[:], ["wf"], T.wti[:], ["wti"])
+    ts(T.wg[:], ["wg"], T.wf[:], ["wf"], 2048.0, OP.is_gt, -4096.0, OP.mult)
+    tt(T.wg[:], ["wg"], T.wg[:], T.wf[:], ["wg", "wf"], OP.add)
+    for nm, val in (("E1", 1.0), ("E8", 8192.0), ("E4n", -4096.0)):
+        ts(T[nm][:], [nm], T.col[:, 0:144], ["col"], T.pg15[:], OP.is_equal, val, OP.mult, cols=["pg15"])
+    ts(T.EW[:], ["EW"], T.E1[:], ["E1"], T.wg[:], OP.mult, cols=["wg"])
+    for nm, val in (("I16", 1.0), ("IB", 1.0), ("IBAR", 16777216.0)):
+        ts(T[nm][:], [nm], T.col[:, 0:128], ["col"], T.pidf[:], OP.is_equal, val, OP.mult, cols=["pidf"])
+    cp(T.qs[:], ["qs"], T.pai[:], ["pai"])
+    cp(T.t2[:], ["t2"], T.pbi[:], ["pbi"])
+    dma("y", "sta", [(T.oad[:], T.qs[:])], ["qs"], ["oad"])
+    dma("y", "stb", [(T.obd[:], T.t2[:])], ["t2"], ["obd"])
+    dma("y", "roa", [(T.OA[m::16, 0:WN], T.oad[:]) for m in range(16)], ["oad"], ["OA"])
+    dma("y", "rob", [(T.OB[m::16, 0:WN], T.obd[:]) for m in range(16)], ["obd"], ["OB"])
+    ts(T.dl[:], ["dl"], T.colL[:], ["colL"], T.pmf[:], OP.is_equal, cols=["pmf"])
+    ts(T.a0[:], ["a0"], T.pgf[:], ["pgf"], 0.0, OP.is_equal)
+    ts(T.a1[:], ["a1"], T.pgf[:], ["pgf"], 1.0, OP.is_equal)
+    ts(T.a1n[:], ["a1n"], T.pgf[:], ["pgf"], 1.0, OP.is_equal, -4096.0, OP.mult)
+    ts(T.q32[:], ["q32"], T.pidf[:], ["pidf"], 32.0, OP.is_equal)
+    ts(T.q32n[:], ["q32n"], T.pidf[:], ["pidf"], 32.0, OP.is_equal, -4096.0, OP.mult)
+    ts(T.q33n[:], ["q33n"], T.pidf[:], ["pidf"], 33.0, OP.is_equal, -4096.0, OP.mult)
+    tt(T.qsn[:], ["qsn"], T.q32n[:], T.q33n[:], ["q32n", "q33n"], OP.add)
+    ts(T.tj[:], ["tj"], T.colJ[:], ["colJ"], T.a1[:], OP.mult, T.a0[:], OP.add, cols=["a1", "a0"])
+    tt(T.tj[:], ["tj"], T.tj[:], T.dl[:], ["tj", "dl"], OP.mult)
+    ts(T.RC[:], ["RC"], T.tj[:], ["tj"], T.q32[:], OP.add, cols=["q32"])
+    ts(T.RL[:], ["RL"], T.dl[:], ["dl"], T.a0[:], OP.mult, cols=["a0"])
+    c0 = 16 * SPLIT
+    ts(T.RO[:, 0:c0], ["RO"], T.dl[:, 0:c0], ["dl"], T.a1n[:], OP.mult, T.qsn[:], OP.add, cols=["a1n", "qsn"])
+    if c0 < 512:
+        ts(T.RO[:, c0:512], ["RO"], T.dl[:, c0:512], ["dl"], 0.0, OP.mult, T.q32n[:], OP.add, cols=["q32n"])
+    ts(T.TA[:], ["TA"], T.col[:, 0:34], ["col"], 0.0, OP.mult)
+    ts(T.TB[:], ["TB"], T.col[:, 0:34], ["col"], 0.0, OP.mult)
+    ts(T.TB[:, 32:33], ["TB"], T.pidf[:], ["pidf"], 0.0, OP.mult, 4088.0, OP.add)
+    ts(T.TB[:, 33:34], ["TB"], T.pidf[:], ["pidf"], 0.0, OP.mult, 2048.0, OP.add)
+
+    def late_constants():
+        ts(T.BO[:], ["BO"], T.colg[:], ["colg"], T.pgf[:], OP.is_equal, cols=["pgf"])
+        ts(T.TRI[:], ["TRI"], T.colL[:, 0:128], ["colL"], T.pmf[:], OP.is_gt, cols=["pmf"])
+        tt(T.TRI[:], ["TRI"], T.TRI[:], T.BO[:], ["TRI", "BO"], OP.mult)
+        ts(T.DM[:], ["DM"], T.colL[:, 0:256], ["colL"], T.pmf[:], OP.is_equal, cols=["pmf"])
+        ts(T.OFFB[:], ["OFFB"], T.colL[:, 0:256], ["colL"], T.pmf[:], OP.not_equal, 16384.0, OP.mult, cols=["pmf"])
+        ts(T.SEG[:], ["SEG"], T.colL[:, 0:256], ["colL"], 0.0, OP.not_equal)
+        ts(T.SEGB[:], ["SEGB"], T.colL[:, 0:256], ["colL"], 0.0, OP.is_equal, 2.0e9, OP.mult)
+        ts(T.SEGB[:], ["SEGB"], T.SEGB[:], ["SEGB"], -1.0e9, OP.add)
+        ts(T.DMD[:], ["DMD"], T.col[:], ["col"], 4097.0, OP.add)
+        tt(T.DMD[:], ["DMD"], T.DMD[:], T.DM[:], ["DMD", "DM"], OP.mult)
+        ts(T.vr0[:], ["vr0"], T.col[:], ["col"], 16.0, OP.mult)
+        ts(T.vr1[:], ["vr1"], T.col[:], ["col"], 16.0, OP.mult, 1.0, OP.add)
+        ts(T.DC[:], ["DC"], T.col[:, 0:16], ["col"], 16.0, OP.mult, T.pmf[:], OP.add, cols=["pmf"])
+        ts(T.DC[:], ["DC"], T.DC[:], ["DC"], 4096.0, OP.add)
+
+    late_constants()
+
+    def run_flags(t, near, dst):
+        ts(T.pm[:], ["pm"], T[near][:, t:WN:16], [near], 0.0, OP.is_ge)
+        tt(T.pm[:], ["pm"], T.pm[:], T.DMD[:], ["pm", "DMD"], OP.mult)
+        scan(T.ps[:], ["ps"], T.SEG[:], T.pm[:], ["SEG", "pm"], 0.0, OP.mult, OP.add)
+        ts(T["DS%d" % t][:], ["DS%d" % t], T.ps[:, 15:256:16], ["ps"], -1.0, OP.add)
+        send("D%d" % t, dst, T["DR%d" % t][:], T["DS%d" % t][:], ["DS%d" % t])
+
+    def near_update(t, near):
+        tab = T[near][:, t:WN:16]
+        tt(tab, [near], T.IOTA[:, 0:WD + 8].indirect(T["PR%d" % t][:]), tab, ["IOTA", "IOTAd", "PR%d" % t, near], OP.max)
+
+    def search(t, d, z, zr, hooks):
+        for l in range(16):
+            mm(T.ph[:, 0:16], ["ph"], T.EW[:, 15 - l:143 - l], z[:, l:256:16], ["EW", zr], l == 0, l == 15)
+        cp(T.ui[:], ["ui"], T.ph[:, 0:16], ["ph"])
+        ts(T.u[:], ["u"], T.ui[:], ["ui"], 4095, OP.bitwise_and)
+        tt(T.sq[:], ["sq"], T.u[:], T.u[:], ["u"], OP.mult)
+        ts(T.TA[:, 16:32], ["TA"], T.u[:], ["u"], -2048.0, OP.add)
+        ts(T.hm[:], ["hm"], T.sq[:], ["sq"], 5, OP.arith_shift_right, 4095, OP.bitwise_and)
+        ts(T.TA[:, 0:16], ["TA"], T.hm[:], ["hm"], -2048.0, OP.add)
+        mm(T.pt[0:33, 0:128], ["pt"], T.TA[:, 0:33], T.I16[:], ["TA", "I16"], True, True)
+        cp(T.TAT[0:33, :], ["TAT"], T.pt[0:33, 0:128], ["pt"])
+        mm(T.pc[:], ["pc"], T.TAT[0:33, :], T.RC[0:33, :], ["TAT", "RC"], True, True)
+        for l in range(16):
+            mm(T.pq[:, 0:16], ["pq"], T.E1[:, 15 - l:143 - l], z[:, l:256:16], ["E1", zr], l == 0, l == 15)
+        for i in range(4):
+            mm(T.pz[:, 256 * i:256 * i + 256], ["pz"], T.IB[:], z[:], ["IB", zr], True, True)
+        for i, (a, b) in enumerate(((0, 128), (128, 512))):
+            cp(T.CI[:, a:b], ["CI%d" % i], T.pc[:, a:b], ["pc"])
+            ts(T.CM[:, a:b], ["CM%d" % i], T.CI[:, a:b], ["CI%d" % i], 4095, OP.bitwise_and)
+            cp(T.LST[:, a:b], ["LST%d" % i], T.CM[:, a:b], ["CM%d" % i])
+        for k, (kind, j0, j1) in enumerate(CH):
+            if kind == "S":
+                act(T.A[:, 256 * j0:256 * j1], ["A%d" % k], T.X[:, 0:WN].indirect(T.LST[:, 16 * j0:16 * j1]), ["X", "LST%d" % (j0 >= 8)], AF.Copy)
+        ts(T.TB[:, 16:32], ["TB"], T.pq[:, 0:16], ["pq"], -2048.0, OP.add)
+        mm(T.pt[0:34, 0:128], ["pt"], T.TB[:], T.I16[:], ["TB", "I16"], True, True)
+        cp(T.TBT[0:34, :], ["TBT"], T.pt[0:34, 0:128], ["pt"])
+        mm(T.pk[:], ["pk"], T.TBT[0:34, :], T.RO[0:34, :], ["TBT", "RO"], True, False)
+        if d > 0:
+            mm(T.pla[:], ["pla"], T.TBT[0:34, :], T.RL[0:34, :], ["TBT", "RL"], True, True)
+        for k, (kind, j0, j1) in enumerate(CH):
+            A, M = T.A[:, 256 * j0:256 * j1], T.M[:, 256 * j0:256 * j1]
+            if kind == "R":
+                for j in range(j0, j1):
+                    tt(T.A[:, 256 * j:256 * j + 256], ["A%d" % k], T.X[:, 0:WN].indirect(T.LST[:, 16 * j:16 * j + 16]), z[:], ["X", "LST1", zr], OP.subtract)
+                ts(M, ["M%d" % k], A, ["A%d" % k], 0.0, OP.max)
+            else:
+                tt(M, ["M%d" % k], A, T.pz[:, 0:256 * (j1 - j0)], ["A%d" % k, "pz"], OP.max)
+            for src, sel in (("A", "E4n"), ("M", "E8")):
+                for l in range(16):
+                    mm(T.pk[:, 16 * j0:16 * j1], ["pk"], T[sel][:, 15 - l:143 - l], T[src][:, 256 * j0 + l:256 * j1:16], [sel, "%s%d" % (src, k)], False, False)
+            if k == 2:
+                ts(T.c16[:], ["c16"], T.LST[:], ["LST0", "LST1"], -2048.0, OP.add)
+                if d > 0:
+                    tt(T.bar[:], ["bar"], T.c16[:], T.pla[:], ["c16", "pla"], OP.is_equal)
+                    mm(T.pk[:], ["pk"], T.IBAR[:], T.bar[:], ["IBAR", "bar"], False, False)
+                else:
+                    ts(T.sm[:], ["sm"], z[:], [zr], -0.5, OP.add)
+            if k == len(CH) - 3:
+                for h in hooks:
+                    h()
+        mm(T.pk[:], ["pk"], T.I16[:], T.c16[:], ["I16", "c16"], False, True)
+        for L in range(16):
+            op("v", g.vector.tensor_reduce, ["pk"], ["ym"], out=T.ym[:, L:L + 1], in_=T.pk[:, L:512:16], axis=AxisListType.X, op=OP.min)
+
+    def pair(t, d, far, kd):
+        xn, l2 = "XN%d" % d, "L2%d" % d
+        dr = "DR%d" % t
+        ts(T.yi[:], ["yi"], T.ym[:], ["ym"], 2048.0, OP.add)
+        ts(T.y[:], ["y"], T.yi[:], ["yi"], 4095, OP.bitwise_and)
+        tt(T.yc[:], ["yc"], T.y[:], T[dr][:], ["y", dr], OP.max)
+        cp(T.yl[:], ["yl"], T.yc[:], ["yc"])
+        ow = T[far][:, 0:WD]
+        act(T.Or[:], ["Or"], ow.indirect(T.yl[:]), [far, far + "d", "yl"], AF.Copy)
+        act(T.XG[:], ["XG"], T.X[:, 0:WD].indirect(T.yl[:]), ["X", "Xd", "yl"], AF.Copy)
+        cp(T.Yr[:], ["Yr"], T.IOTA[:, 0:WD].indirect(T.yl[:]), ["IOTA", "yl"])
+        mm(T.pq[:, 0:256], ["pq"], T.IB[:], T.OFFB[:], ["IB", "OFFB"], True, False)
+        mm(T.pq[:, 0:256], ["pq"], T.IB[:], T.Or[:], ["IB", "Or"], False, False)
+        base = 0
+        for L in range(16):
+            n = 256 - 16 * L
+            e = "EQ%d" % L
+            ts(T.EQ[:, base:base + n], [e], T.Yr[:, 16 * L:256], ["Yr"], T.yc[:, L:L + 1], OP.is_equal, cols=["yc"])
+            if n > 16:
+                mm(T.pq[:, 16 * L + 16:256], ["pq"], T.BO[:], T.EQ[:, base + 16:base + n], ["BO", e], False, False)
+            if L == 10:
+                mm(T.ph[:, 0:256], ["ph"], T.IB[:], T.XG[:], ["IB", "XG"], True, False)
+                mm(T.ph[:, 0:256], ["ph"], T.I16[:], T.sm[:], ["I16", "sm"], False, True)
+            mm(T.pq[:, 16 * L:16 * L + 16], ["pq"], T.TRI[:], T.EQ[:, base:base + 16], ["TRI", e], False, L == 15)
+            base += n
+        act(T.t2[:], ["t2"], T.ph[:, 0:256], ["ph"], AF.Copy, bias=8388608.0, scale=0.5)
+        act(T[xn][:], [xn], T.t2[:], ["t2"], AF.Copy, bias=-8388608.0)
+        tell = d < STEPS - 1
+        dst = up if t == 0 else down
+        if tell:
+            send("X%d%d" % (t, d), dst, T["XI%d%d" % (t, d)][:], T[xn][:], [xn])
+        scan(T.qs[:], ["qs"], T.SEGB[:], T.pq[:, 0:256], ["SEGB", "pq"], 1.0e9, OP.max, OP.min)
+        ts(T.nw[:], ["nw"], T.qs[:, 15:256:16], ["qs"], 0.0, OP.is_ge, 8192.0, OP.mult)
+        tt(T.yw[:], ["yw"], T.yc[:], T.nw[:], ["yc", "nw"], OP.add)
+        tt(T.lf[:], ["lf"], T.yw[:], T.DC[:], ["yw", "DC"], OP.min)
+        cp(T[l2][:], [l2], T.lf[:], ["lf"])
+        if tell:
+            send("L%d%d" % (t, d), dst, T["LI%d%d" % (t, d)][:], T[l2][:], [l2])
+
+        def home():
+            tt(T.PLf[:], ["PLf"], T.PLf[:], T.yw[:], ["PLf", "yw"], OP.min)
+            if d == STEPS - 1:
+                ts(T.lf[:], ["lf"], T.PLf[:], ["PLf"], float(WD), OP.min)
+                cp(T["PS%d" % t][:], ["PS%d" % t], T.lf[:], ["lf"])
+                fill(T.PLf[:], "PLf", 8192.0)
+
+        def put_records():
+            cp(T.X[:, 0:WD].indirect(T[l2][:]), ["X", "Xd"], T[xn][:], [xn, l2])
+
+        def put_far():
+            cp(ow.indirect(T[l2][:]), [far, far + "d"], T["vr%d" % t][:], ["vr%d" % t, l2])
+
+        def small():
+            ts(T.wb[:], ["wb"], T.nw[:], ["nw"], 0.0, OP.is_equal)
+            mm(T.pt[:, 0:16], ["pt"], T.ONES[:], T.wb[:], ["ONES", "wb"], True, True)
+            if tell:
+                tt(T.wd[:], ["wd"], T.wb[:], T.DC[:], ["wb", "DC"], OP.mult)
+                tt(T[dr][:], [dr], T[dr][:], T.wd[:], [dr, "wd"], OP.max)
+                ts(T.TB[:, 0:16], ["TB"], T.y[:], ["y"], -2048.0, OP.add)
+            op("v", g.vector.tensor_reduce, ["pt"], ["kf"], out=T.kf[:], in_=T.pt[:, 0:16], axis=AxisListType.X, op=OP.add)
+            cp(T.ki[:], ["ki"], T.kf[:], ["kf"])
+            ts(T.ka[:], ["ka"], T.ki[:], ["ki"], 31, OP.bitwise_and)
+            ts(T.TA[:, 32:33], ["TA"], T.ka[:], ["ka"], float(kd), OP.add)
+
+        return home, put_records, put_far, small
+
+    def next_z(t, d, far):
+        src = down if t == 0 else up
+        xr = "XR%d" % t
+        arrives("X%d%d" % (t, d), src, "XI%d%d" % (t, d))
+        arrives("L%d%d" % (t, d), src, "LI%d%d" % (t, d))
+        cp(T[xr][:, 0:WD].indirect(T["LI%d%d" % (t, d)][:]), [xr], T["XI%d%d" % (t, d)][:], [xr, "XI%d%d" % (t, d), "LI%d%d" % (t, d)])
+        cp(T.zb[:], ["zb"], T[xr][:, 0:WN].indirect(T.pl16[:]), [xr, "pl16"])
+
+    for t in range(2):
+        far = "OB" if t == 0 else "OA"
+        near = "OA" if t == 0 else "OB"
+        for d in range(STEPS):
+            hooks = []
+            if (t, d) == (0, 0):
+                hooks.append(lambda: run_flags(0, "OA", up))
+                hooks.append(lambda: arrives("D0", down, "DR0"))
+            if (t, d) == (1, 0):
+                hooks.append(lambda: near_update(0, "OA"))
+            zn = "SR%d" % t if d == 0 else "zb"
+            search(t, d, T[zn], zn, hooks)
+            home, put_records, put_far, small = pair(t, d, far, 97 * (d + 1) if d < STEPS - 1 else 0)
+            if d < STEPS - 1:
+                put_far()
+                tt(T.pm[:], ["pm"], T[far][:, 0:WD].indirect(T.yl[:]), T.DM[:], [far, far + "d", "yl", "DM"], OP.mult)
+                scan(T.ps[:], ["ps"], T.SEG[:], T.pm[:], ["SEG", "pm"], 0.0, OP.mult, OP.add)
+                cp(T.pl16[:], ["pl16"], T.ps[:, 15:256:16], ["ps"])
+                put_records()
+                home()
+                small()
+                next_z(t, d, far)
+            elif t == 0:
+                put_records()
+                send_starts(1, down)
+                put_far()
+                home()
+                send("P0", down, T.PR0[:], T.PS0[:], ["PS0"])
+                run_flags(1, "OB", down)
+                small()
+                arrives("S1", up, "SR1")
+                arrives("B1", up, "XR1")
+                arrives("D1", up, "DR1")
+                arrives("P0", up, "PR0")
+            else:
+                home()
+                send("P1", up, T.PR1[:], T.PS1[:], ["PS1"])
+                arrives("P1", down, "PR1")
+                put_records()
+                dma("y", "outx", [(T.yx[:], T.X[:, 0:WN])], ["X"], [])
+                put_far()
+                dma("y", "outa", [(T.ya[:], T.OA[0:128:16, 0:WN])], ["OA"], [])
+                near_update(1, "OB")
+                dma("y", "outb", [(T.yb[:], T.OB[0:128:16, 0:WN])], ["OB"], [])
+    for sem in sorted(count):
+        wait("g", [("", sem, count[sem])])

@@ -4,8 +4,10 @@ N = 5
 WN = 4096
 WD = 4352
 STEPS = 3
-CH = [("S", 0, 4), ("S", 4, 8), ("R", 28, 32), ("S", 8, 12), ("S", 12, 16), ("S", 16, 20), ("S", 20, 24), ("S", 24, 26), ("S", 26, 28)]
-SPLIT = 28
+NR = 4
+SCH = [[(4, 8)], [(8, 12)], [(12, 16)], [(16, 20)], [(20, 24)], [(24, 28)], [(28, 30), (30, 32)]]
+EARLY = 3
+PORTIONS = ((0, 128, "pc", "pt"), (128, 512, "pla", "ph"))
 
 SCRATCH = {}
 for _n, _c, _d in (
@@ -13,18 +15,18 @@ for _n, _c, _d in (
         ("IOTA", WD + 8, "float32"), ("A", 8192, "bfloat16"), ("M", 8192, "bfloat16"), ("zb", 256, "bfloat16"),
         ("pai", 256, "int32"), ("pbi", 256, "int32"), ("wti", 1, "int32"), ("wf", 1, "float32"), ("wg", 1, "float32"),
         ("pidx", 1, "int32"), ("pmi", 1, "int32"), ("pgi", 1, "int32"), ("pidf", 1, "float32"), ("pmf", 1, "float32"), ("pgf", 1, "float32"), ("pg15", 1, "float32"),
-        ("a0", 1, "float32"), ("a1", 1, "float32"), ("a1n", 1, "float32"), ("q32", 1, "float32"), ("q32n", 1, "float32"), ("q33n", 1, "float32"), ("qsn", 1, "float32"),
-        ("col", 256, "float32"), ("colL", 512, "float32"), ("colJ", 512, "float32"), ("colg", 128, "float32"), ("dl", 512, "float32"), ("tj", 512, "float32"),
-        ("E1", 144, "bfloat16"), ("E8", 144, "bfloat16"), ("E4n", 144, "bfloat16"), ("EW", 144, "float16"),
-        ("I16", 128, "float16"), ("IB", 128, "bfloat16"), ("IBAR", 128, "bfloat16"), ("BO", 128, "bfloat16"), ("TRI", 128, "bfloat16"), ("ONES", 128, "bfloat16"),
+        ("kc", 8, "float32"),
+        ("col", 256, "float32"), ("colL", 512, "float32"), ("colJ", 512, "float32"), ("colg", 128, "float32"), ("dl", 512, "float32"),
+        ("E8", 144, "bfloat16"), ("E4n", 144, "bfloat16"), ("WG", 8, "float16"), ("GS", 8, "bfloat16"), ("CK", 2, "bfloat16"),
+        ("I16", 128, "float16"), ("IB", 128, "bfloat16"), ("IB8", 128, "bfloat16"), ("INB", 128, "bfloat16"), ("IBAR", 128, "bfloat16"), ("BO", 128, "bfloat16"), ("TRI", 128, "bfloat16"), ("ONE", 512, "bfloat16"),
         ("DM", 256, "float32"), ("DMD", 256, "float32"), ("OFFB", 256, "bfloat16"), ("SEG", 256, "float32"), ("SEGB", 256, "float32"),
-        ("RC", 512, "float16"), ("RL", 512, "float16"), ("RO", 512, "float16"), ("vr0", 256, "float32"), ("vr1", 256, "float32"), ("DC", 16, "float32"),
-        ("ui", 16, "int32"), ("u", 16, "int32"), ("sq", 16, "int32"), ("hm", 16, "int32"), ("TA", 34, "float16"), ("TB", 34, "float16"), ("TAT", 128, "float16"), ("TBT", 128, "float16"),
-        ("CI", 512, "int32"), ("CM", 512, "int32"), ("LST", 512, "uint16"), ("c16", 512, "float16"), ("bar", 512, "bfloat16"),
+        ("RH", 512, "float16"), ("RU", 512, "float16"), ("RZ", 512, "float16"), ("RK", 512, "bfloat16"), ("RO", 512, "bfloat16"), ("KC", 128, "bfloat16"), ("KT", 128, "bfloat16"), ("vr0", 256, "float32"), ("vr1", 256, "float32"), ("DC", 16, "float32"),
+        ("ui", 128, "int32"), ("u", 128, "int32"), ("sq", 128, "int32"), ("hm", 128, "int32"), ("UT", 128, "float16"), ("HT", 128, "float16"), ("ZT", 128, "float16"), ("LT", 128, "float16"), ("TB", 16, "float16"),
+        ("RR", 512, "bfloat16"), ("LST", 512, "uint16"), ("c16", 512, "float16"), ("bar", 512, "bfloat16"),
         ("ym", 16, "float32"), ("yi", 16, "int32"), ("y", 16, "int32"), ("yc", 16, "float32"), ("yl", 16, "uint16"), ("Yr", 256, "uint16"), ("Or", 256, "bfloat16"),
-        ("XG", 256, "bfloat16"), ("sm", 256, "float16"), ("t2", 256, "float32"), ("EQ", 2176, "bfloat16"), ("qs", 256, "float32"), ("nw", 16, "float32"), ("yw", 16, "float32"),
+        ("XG", 256, "bfloat16"), ("sm", 256, "float16"), ("t2", 256, "float32"), ("qs", 256, "float32"), ("nw", 16, "float32"), ("EQ", 2176, "bfloat16"),
         ("lf", 16, "float32"), ("pm", 256, "float32"), ("ps", 256, "float32"), ("pl16", 16, "uint16"), ("PLf", 16, "float32"), ("wb", 16, "bfloat16"), ("wd", 16, "float32"),
-        ("kf", 1, "float32"), ("ki", 1, "int32"), ("ka", 1, "int32")):
+        ("k1", 1, "float32"), ("kr", 1, "float32"), ("kf", 1, "float32")):
     SCRATCH[_n] = ("sbuf", [128, _c], _d)
 for _t in range(2):
     for _n, _c, _d in (("SS", 256, "bfloat16"), ("SR", 256, "bfloat16"), ("DS", 16, "float32"), ("DR", 16, "float32"), ("PS", 16, "uint16"), ("PR", 16, "uint16")):
@@ -39,7 +41,7 @@ SCRATCH["oad"] = ("dram", [8, WN], "float32")
 SCRATCH["obd"] = ("dram", [8, WN], "float32")
 for _n, _c in (("pz", 1024), ("ph", 512), ("pt", 512), ("pc", 512), ("pla", 512), ("pk", 512), ("pq", 512)):
     SCRATCH[_n] = ("psum", [128, _c], "float32")
-PARTS = ("ym", "RO", "TA", "A2")
+PARTS = ("ym", "RO", "RZ", "A0")
 PSUM = ("pz", "ph", "pt", "pc", "pla", "pk", "pq")
 
 MSG = []
@@ -139,7 +141,7 @@ def rank_program(g, core, T, topo):
 
     up, down = T.cores[(me + 1) % N], T.cores[(me - 1) % N]
 
-    dma("y", "ldx", [(T.X[:, 0:WN], T.x[:])], [], ["X"])
+    dma("s", "ldx", [(T.X[:, 0:WN], T.x[:])], [], ["X"])
     dma("y", "ldw", [(T.wti[:], T.wt[:])], [], ["wti"])
     dma("y", "lda", [(T.pai[:], T.pa[:])], [], ["pai"])
     dma("y", "ldb", [(T.pbi[:], T.pb[:])], [], ["pbi"])
@@ -176,7 +178,9 @@ def rank_program(g, core, T, topo):
     fill(T.OA[:, WN:WD], "OAd", 0.0)
     fill(T.OB[:, WN:WD], "OBd", 0.0)
     fill(T.IOTA[:, WD:WD + 8], "IOTAd", -1.0)
-    fill(T.ONES[:], "ONES", 1.0)
+    fill(T.ONE[:], "ONE", 1.0)
+    fill(T.KT[:], "KT", 0.0)
+    fill(T.CK[:], "CK", -15.5 / 128)
     fill(T.PLf[:], "PLf", 8192.0)
     ts(T.pmi[:], ["pmi"], T.pidx[:], ["pidx"], 15, OP.bitwise_and)
     ts(T.pgi[:], ["pgi"], T.pidx[:], ["pidx"], 4, OP.arith_shift_right)
@@ -184,50 +188,53 @@ def rank_program(g, core, T, topo):
     cp(T.pmf[:], ["pmf"], T.pmi[:], ["pmi"])
     cp(T.pgf[:], ["pgf"], T.pgi[:], ["pgi"])
     ts(T.pg15[:], ["pg15"], T.pgf[:], ["pgf"], 16.0, OP.mult, 15.0, OP.add)
+    for nm, val in (("E8", 8192.0), ("E4n", -4096.0)):
+        ts(T[nm][:], [nm], T.col[:, 0:144], ["col"], T.pg15[:], OP.is_equal, val, OP.mult, cols=["pg15"])
+    ts(T.GS[:], ["GS"], T.col[:, 0:8], ["col"], T.pgf[:], OP.is_equal, cols=["pgf"])
+    for nm, val in (("I16", 1.0), ("IB", 1.0), ("INB", -1.0), ("IBAR", 16777216.0)):
+        ts(T[nm][:], [nm], T.col[:, 0:128], ["col"], T.pidf[:], OP.is_equal, val, OP.mult, cols=["pidf"])
+    ts(T.dl[:], ["dl"], T.colL[:], ["colL"], T.pmf[:], OP.is_equal, cols=["pmf"])
+    cp(T.RH[:], ["RH"], T.dl[:], ["dl"])
+    tt(T.RU[:], ["RU"], T.colJ[:], T.dl[:], ["colJ", "dl"], OP.mult)
+    h0, g1, g3, e1, r1, r2, kv, rv = [T.kc[:, i:i + 1] for i in range(8)]
+    ts(h0, ["h0"], T.pidf[:], ["pidf"], 0.0, OP.is_equal, 0.5, OP.mult)
+    ts(g1, ["g1"], T.pidf[:], ["pidf"], 1.0, OP.is_ge, 2048.0, OP.mult)
+    ts(g3, ["g3"], T.pidf[:], ["pidf"], 3.0, OP.is_ge, -8.0, OP.mult)
+    ts(e1, ["e1"], T.pidf[:], ["pidf"], 1.0, OP.is_equal, -1.0, OP.mult)
+    ts(r1, ["r1"], T.pidf[:], ["pidf"], 1.0, OP.is_ge, -4096.0, OP.mult)
+    ts(r2, ["r2"], T.pidf[:], ["pidf"], 2.0, OP.is_ge, -4096.0, OP.mult)
+    tt(kv, ["kv"], h0, g1, ["h0", "g1"], OP.add)
+    ts(rv, ["rv"], T.pidf[:], ["pidf"], 0.0, OP.is_equal, e1, OP.add, cols=["e1"])
+    tt(kv, ["kv"], kv, g3, ["kv", "g3"], OP.add)
+    ts(T.RK[:], ["RK"], T.ONE[:], ["ONE"], rv, OP.mult, cols=["rv"])
+    ts(T.KC[:], ["KC"], T.ONE[:, 0:128], ["ONE"], kv, OP.mult, cols=["kv"])
     cp(T.wf[:], ["wf"], T.wti[:], ["wti"])
     ts(T.wg[:], ["wg"], T.wf[:], ["wf"], 2048.0, OP.is_gt, -4096.0, OP.mult)
     tt(T.wg[:], ["wg"], T.wg[:], T.wf[:], ["wg", "wf"], OP.add)
-    for nm, val in (("E1", 1.0), ("E8", 8192.0), ("E4n", -4096.0)):
-        ts(T[nm][:], [nm], T.col[:, 0:144], ["col"], T.pg15[:], OP.is_equal, val, OP.mult, cols=["pg15"])
-    ts(T.EW[:], ["EW"], T.E1[:], ["E1"], T.wg[:], OP.mult, cols=["wg"])
-    for nm, val in (("I16", 1.0), ("IB", 1.0), ("IBAR", 16777216.0)):
-        ts(T[nm][:], [nm], T.col[:, 0:128], ["col"], T.pidf[:], OP.is_equal, val, OP.mult, cols=["pidf"])
+    ts(T.WG[:], ["WG"], T.GS[:], ["GS"], T.wg[:], OP.mult, cols=["wg"])
+    c0 = 16 * NR
+    ts(T.RO[:, c0:512], ["RO"], T.ONE[:, c0:512], ["ONE"], r1, OP.mult, cols=["r1"])
+    ts(T.RO[:, 0:c0], ["RO"], T.ONE[:, 0:c0], ["ONE"], r2, OP.mult, cols=["r2"])
+    ts(T.RZ[:, c0:512], ["RZ"], T.RH[:, c0:512], ["RH"], -4096.0, OP.mult)
+    ts(T.RZ[:, 0:c0], ["RZ"], T.RH[:, 0:c0], ["RH"], 0.0, OP.mult)
     cp(T.qs[:], ["qs"], T.pai[:], ["pai"])
     cp(T.t2[:], ["t2"], T.pbi[:], ["pbi"])
     dma("y", "sta", [(T.oad[:], T.qs[:])], ["qs"], ["oad"])
     dma("y", "stb", [(T.obd[:], T.t2[:])], ["t2"], ["obd"])
     dma("y", "roa", [(T.OA[m::16, 0:WN], T.oad[:]) for m in range(16)], ["oad"], ["OA"])
     dma("y", "rob", [(T.OB[m::16, 0:WN], T.obd[:]) for m in range(16)], ["obd"], ["OB"])
-    ts(T.dl[:], ["dl"], T.colL[:], ["colL"], T.pmf[:], OP.is_equal, cols=["pmf"])
-    ts(T.a0[:], ["a0"], T.pgf[:], ["pgf"], 0.0, OP.is_equal)
-    ts(T.a1[:], ["a1"], T.pgf[:], ["pgf"], 1.0, OP.is_equal)
-    ts(T.a1n[:], ["a1n"], T.pgf[:], ["pgf"], 1.0, OP.is_equal, -4096.0, OP.mult)
-    ts(T.q32[:], ["q32"], T.pidf[:], ["pidf"], 32.0, OP.is_equal)
-    ts(T.q32n[:], ["q32n"], T.pidf[:], ["pidf"], 32.0, OP.is_equal, -4096.0, OP.mult)
-    ts(T.q33n[:], ["q33n"], T.pidf[:], ["pidf"], 33.0, OP.is_equal, -4096.0, OP.mult)
-    tt(T.qsn[:], ["qsn"], T.q32n[:], T.q33n[:], ["q32n", "q33n"], OP.add)
-    ts(T.tj[:], ["tj"], T.colJ[:], ["colJ"], T.a1[:], OP.mult, T.a0[:], OP.add, cols=["a1", "a0"])
-    tt(T.tj[:], ["tj"], T.tj[:], T.dl[:], ["tj", "dl"], OP.mult)
-    ts(T.RC[:], ["RC"], T.tj[:], ["tj"], T.q32[:], OP.add, cols=["q32"])
-    ts(T.RL[:], ["RL"], T.dl[:], ["dl"], T.a0[:], OP.mult, cols=["a0"])
-    c0 = 16 * SPLIT
-    ts(T.RO[:, 0:c0], ["RO"], T.dl[:, 0:c0], ["dl"], T.a1n[:], OP.mult, T.qsn[:], OP.add, cols=["a1n", "qsn"])
-    if c0 < 512:
-        ts(T.RO[:, c0:512], ["RO"], T.dl[:, c0:512], ["dl"], 0.0, OP.mult, T.q32n[:], OP.add, cols=["q32n"])
-    ts(T.TA[:], ["TA"], T.col[:, 0:34], ["col"], 0.0, OP.mult)
-    ts(T.TB[:], ["TB"], T.col[:, 0:34], ["col"], 0.0, OP.mult)
-    ts(T.TB[:, 32:33], ["TB"], T.pidf[:], ["pidf"], 0.0, OP.mult, 4088.0, OP.add)
-    ts(T.TB[:, 33:34], ["TB"], T.pidf[:], ["pidf"], 0.0, OP.mult, 2048.0, OP.add)
 
     def late_constants():
-        ts(T.BO[:], ["BO"], T.colg[:], ["colg"], T.pgf[:], OP.is_equal, cols=["pgf"])
+        ts(T.IB8[:], ["IB8"], T.IB[:], ["IB"], 8192.0, OP.mult)
+        ts(T.BO[:], ["BO"], T.colg[:], ["colg"], T.pgf[:], OP.is_equal, 8192.0, OP.mult, cols=["pgf"])
         ts(T.TRI[:], ["TRI"], T.colL[:, 0:128], ["colL"], T.pmf[:], OP.is_gt, cols=["pmf"])
         tt(T.TRI[:], ["TRI"], T.TRI[:], T.BO[:], ["TRI", "BO"], OP.mult)
         ts(T.DM[:], ["DM"], T.colL[:, 0:256], ["colL"], T.pmf[:], OP.is_equal, cols=["pmf"])
-        ts(T.OFFB[:], ["OFFB"], T.colL[:, 0:256], ["colL"], T.pmf[:], OP.not_equal, 16384.0, OP.mult, cols=["pmf"])
+        ts(T.OFFB[:], ["OFFB"], T.colL[:, 0:256], ["colL"], T.pmf[:], OP.not_equal, 1073741824.0, OP.mult, cols=["pmf"])
+        ts(T.OFFB[:], ["OFFB"], T.OFFB[:], ["OFFB"], 8192.0, OP.add)
         ts(T.SEG[:], ["SEG"], T.colL[:, 0:256], ["colL"], 0.0, OP.not_equal)
-        ts(T.SEGB[:], ["SEGB"], T.colL[:, 0:256], ["colL"], 0.0, OP.is_equal, 2.0e9, OP.mult)
-        ts(T.SEGB[:], ["SEGB"], T.SEGB[:], ["SEGB"], -1.0e9, OP.add)
+        ts(T.SEGB[:], ["SEGB"], T.colL[:, 0:256], ["colL"], 0.0, OP.is_equal, 2.0e10, OP.mult)
+        ts(T.SEGB[:], ["SEGB"], T.SEGB[:], ["SEGB"], -1.0e10, OP.add)
         ts(T.DMD[:], ["DMD"], T.col[:], ["col"], 4097.0, OP.add)
         tt(T.DMD[:], ["DMD"], T.DMD[:], T.DM[:], ["DMD", "DM"], OP.mult)
         ts(T.vr0[:], ["vr0"], T.col[:], ["col"], 16.0, OP.mult)
@@ -250,55 +257,105 @@ def rank_program(g, core, T, topo):
 
     def search(t, d, z, zr, hooks):
         for l in range(16):
-            mm(T.ph[:, 0:16], ["ph"], T.EW[:, 15 - l:143 - l], z[:, l:256:16], ["EW", zr], l == 0, l == 15)
-        cp(T.ui[:], ["ui"], T.ph[:, 0:16], ["ph"])
-        ts(T.u[:], ["u"], T.ui[:], ["ui"], 4095, OP.bitwise_and)
-        tt(T.sq[:], ["sq"], T.u[:], T.u[:], ["u"], OP.mult)
-        ts(T.TA[:, 16:32], ["TA"], T.u[:], ["u"], -2048.0, OP.add)
-        ts(T.hm[:], ["hm"], T.sq[:], ["sq"], 5, OP.arith_shift_right, 4095, OP.bitwise_and)
-        ts(T.TA[:, 0:16], ["TA"], T.hm[:], ["hm"], -2048.0, OP.add)
-        mm(T.pt[0:33, 0:128], ["pt"], T.TA[:, 0:33], T.I16[:], ["TA", "I16"], True, True)
-        cp(T.TAT[0:33, :], ["TAT"], T.pt[0:33, 0:128], ["pt"])
-        mm(T.pc[:], ["pc"], T.TAT[0:33, :], T.RC[0:33, :], ["TAT", "RC"], True, True)
+            mm(T.ph[0:16, l:128:16], ["ph"], z[:, l:256:16], T.WG[:], ["WG", zr], True, True)
         for l in range(16):
-            mm(T.pq[:, 0:16], ["pq"], T.E1[:, 15 - l:143 - l], z[:, l:256:16], ["E1", zr], l == 0, l == 15)
+            mm(T.pq[0:16, l:128:16], ["pq"], z[:, l:256:16], T.GS[:], ["GS", zr], True, True)
+
+        def raw1(a, b, bank):
+            mm(T[bank][:, a:b], [bank], T.KC[0:4, :], T.RK[0:4, a:b], ["KC", "RK"], True, False)
+            mm(T[bank][:, a:b], [bank], T.KT[0:1, :], T.ONE[0:1, a:b], ["KT", "ONE"], False, False)
+
+        def raw2(a, b, bank):
+            mm(T[bank][:, a:b], [bank], T.UT[0:16, :], T.RU[0:16, a:b], ["UT", "RU"], False, False)
+
+        def raw3(a, b, bank, stop):
+            mm(T[bank][:, a:b], [bank], T.HT[0:16, :], T.RH[0:16, a:b], ["HT", "RH"], False, stop)
+
+        (a0, b0, s0, e0), (a1, b1, s1, e1) = PORTIONS
+        raw1(a0, b0, s0)
+        raw1(a1, b1, s1)
+        raw1(a0, b0, e0)
+        cp(T.ui[0:16, :], ["ui"], T.ph[0:16, 0:128], ["ph"])
+        ts(T.u[0:16, :], ["u"], T.ui[0:16, :], ["ui"], 4095, OP.bitwise_and)
+        tt(T.sq[0:16, :], ["sq"], T.u[0:16, :], T.u[0:16, :], ["u"], OP.mult)
+        ts(T.UT[0:16, :], ["UT"], T.u[0:16, :], ["u"], -2048.0, OP.add)
+        ts(T.hm[0:16, :], ["hm"], T.sq[0:16, :], ["sq"], 5, OP.arith_shift_right, 4095, OP.bitwise_and)
+        ts(T.HT[0:16, :], ["HT"], T.hm[0:16, :], ["hm"], -2048.0, OP.add)
+        raw2(a0, b0, s0)
+        raw2(a1, b1, s1)
+        raw2(a0, b0, e0)
+        raw3(a0, b0, s0, True)
+        raw3(a0, b0, e0, False)
+        raw3(a1, b1, s1, True)
+
+        def near(i):
+            a, b, bank, rest = PORTIONS[i]
+            ts(T.RR[:, a:b], ["RR%d" % i], T[bank][:, a:b], [bank], 51539607552.0, OP.add, -51539607552.0, OP.add)
+            mm(T[rest][:, a:b], [rest], T.INB[:], T.RR[:, a:b], ["INB", "RR%d" % i], False, True)
+
+        def lists(i):
+            a, b, _, rest = PORTIONS[i]
+            ts(T.LST[:, a:b], ["LST%d" % i], T[rest][:, a:b], [rest], 2047.5, OP.add)
+
+        near(0)
+        raw1(a1, b1, e1)
+        raw2(a1, b1, e1)
+        raw3(a1, b1, e1, False)
+        ts(T.ZT[0:16, :], ["ZT"], T.pq[0:16, 0:128], ["pq"], -2048.0, OP.add)
         for i in range(4):
             mm(T.pz[:, 256 * i:256 * i + 256], ["pz"], T.IB[:], z[:], ["IB", zr], True, True)
-        for i, (a, b) in enumerate(((0, 128), (128, 512))):
-            cp(T.CI[:, a:b], ["CI%d" % i], T.pc[:, a:b], ["pc"])
-            ts(T.CM[:, a:b], ["CM%d" % i], T.CI[:, a:b], ["CI%d" % i], 4095, OP.bitwise_and)
-            cp(T.LST[:, a:b], ["LST%d" % i], T.CM[:, a:b], ["CM%d" % i])
-        for k, (kind, j0, j1) in enumerate(CH):
-            if kind == "S":
-                act(T.A[:, 256 * j0:256 * j1], ["A%d" % k], T.X[:, 0:WN].indirect(T.LST[:, 16 * j0:16 * j1]), ["X", "LST%d" % (j0 >= 8)], AF.Copy)
-        ts(T.TB[:, 16:32], ["TB"], T.pq[:, 0:16], ["pq"], -2048.0, OP.add)
-        mm(T.pt[0:34, 0:128], ["pt"], T.TB[:], T.I16[:], ["TB", "I16"], True, True)
-        cp(T.TBT[0:34, :], ["TBT"], T.pt[0:34, 0:128], ["pt"])
-        mm(T.pk[:], ["pk"], T.TBT[0:34, :], T.RO[0:34, :], ["TBT", "RO"], True, False)
+        lists(0)
+        near(1)
+        win = T.X[:, 0:WN]
+        for pieces in SCH:
+            for j0, j1 in pieces:
+                if 16 * j1 <= PORTIONS[0][1]:
+                    act(T.A[:, 256 * j0:256 * j1], ["A%d" % j0], win.indirect(T.LST[:, 16 * j0:16 * j1]), ["X", "LST0"], AF.Copy)
+        mm(T.pk[:], ["pk"], T.KC[0:4, :], T.RO[0:4, :], ["KC", "RO"], True, False)
+        mm(T.pk[:], ["pk"], T.ZT[0:16, :], T.RZ[0:16, :], ["ZT", "RZ"], False, False)
         if d > 0:
-            mm(T.pla[:], ["pla"], T.TBT[0:34, :], T.RL[0:34, :], ["TBT", "RL"], True, True)
-        for k, (kind, j0, j1) in enumerate(CH):
-            A, M = T.A[:, 256 * j0:256 * j1], T.M[:, 256 * j0:256 * j1]
-            if kind == "R":
-                for j in range(j0, j1):
-                    tt(T.A[:, 256 * j:256 * j + 256], ["A%d" % k], T.X[:, 0:WN].indirect(T.LST[:, 16 * j:16 * j + 16]), z[:], ["X", "LST1", zr], OP.subtract)
-                ts(M, ["M%d" % k], A, ["A%d" % k], 0.0, OP.max)
-            else:
-                tt(M, ["M%d" % k], A, T.pz[:, 0:256 * (j1 - j0)], ["A%d" % k, "pz"], OP.max)
-            for src, sel in (("A", "E4n"), ("M", "E8")):
-                for l in range(16):
-                    mm(T.pk[:, 16 * j0:16 * j1], ["pk"], T[sel][:, 15 - l:143 - l], T[src][:, 256 * j0 + l:256 * j1:16], [sel, "%s%d" % (src, k)], False, False)
-            if k == 2:
-                ts(T.c16[:], ["c16"], T.LST[:], ["LST0", "LST1"], -2048.0, OP.add)
-                if d > 0:
-                    tt(T.bar[:], ["bar"], T.c16[:], T.pla[:], ["c16", "pla"], OP.is_equal)
-                    mm(T.pk[:], ["pk"], T.IBAR[:], T.bar[:], ["IBAR", "bar"], False, False)
-                else:
-                    ts(T.sm[:], ["sm"], z[:], [zr], -0.5, OP.add)
-            if k == len(CH) - 3:
+            mm(T.pc[:], ["pc"], T.LT[0:16, :], T.RH[0:16, :], ["LT", "RH"], True, True)
+
+        def sums(src, sel, pieces):
+            j0, j1 = pieces[0][0], pieces[-1][1]
+            for l in range(16):
+                mm(T.pk[:, 16 * j0:16 * j1], ["pk"], T[sel][:, 15 - l:143 - l], T[src][:, 256 * j0 + l:256 * j1:16], [sel] + ["%s%d" % (src, a) for a, _ in pieces], False, False)
+
+        if NR:
+            for j in range(NR):
+                if j == NR // 2:
+                    lists(1)
+                    for pieces in SCH:
+                        for j0, j1 in pieces:
+                            if 16 * j1 > PORTIONS[0][1]:
+                                act(T.A[:, 256 * j0:256 * j1], ["A%d" % j0], win.indirect(T.LST[:, 16 * j0:16 * j1]), ["X", "LST1"], AF.Copy)
+                tt(T.A[:, 256 * j:256 * j + 256], ["A0"], win.indirect(T.LST[:, 16 * j:16 * j + 16]), z[:], ["X", "LST0", zr], OP.subtract)
+            ts(T.M[:, 0:256 * NR], ["M0"], T.A[:, 0:256 * NR], ["A0"], 0.0, OP.max)
+        sums("A", "E4n", SCH[0])
+        if NR:
+            sums("A", "E4n", [(0, NR)])
+            sums("M", "E8", [(0, NR)])
+        ts(T.c16[:], ["c16"], T.LST[:], ["LST0", "LST1"], -2048.0, OP.add)
+        if d > 0:
+            tt(T.bar[:], ["bar"], T.c16[:], T.pc[:], ["c16", "pc"], OP.is_equal)
+        else:
+            ts(T.sm[:], ["sm"], z[:], [zr], -0.5, OP.add)
+        for k, pieces in enumerate(SCH):
+            for j0, j1 in pieces:
+                tt(T.M[:, 256 * j0:256 * j1], ["M%d" % j0], T.A[:, 256 * j0:256 * j1], T.pz[:, 0:256 * (j1 - j0)], ["A%d" % j0, "pz"], OP.max)
+            if k == 0 and d > 0:
+                mm(T.pk[:], ["pk"], T.IBAR[:], T.bar[:], ["IBAR", "bar"], False, False)
+            if k < EARLY:
+                sums("A", "E4n", SCH[k + 1])
+            sums("M", "E8", pieces)
+            if k == len(SCH) - 2:
+                mm(T.pk[:, 0:16 * SCH[-1][0][0]], ["pk"], T.I16[:], T.c16[:, 0:16 * SCH[-1][0][0]], ["I16", "c16"], False, False)
+            if EARLY <= k < len(SCH) - 1:
+                sums("A", "E4n", SCH[k + 1])
+            if k == 4:
                 for h in hooks:
                     h()
-        mm(T.pk[:], ["pk"], T.I16[:], T.c16[:], ["I16", "c16"], False, True)
+        mm(T.pk[:, 16 * SCH[-1][0][0]:512], ["pk"], T.I16[:], T.c16[:, 16 * SCH[-1][0][0]:512], ["I16", "c16"], False, True)
         for L in range(16):
             op("v", g.vector.tensor_reduce, ["pk"], ["ym"], out=T.ym[:, L:L + 1], in_=T.pk[:, L:512:16], axis=AxisListType.X, op=OP.min)
 
@@ -310,11 +367,14 @@ def rank_program(g, core, T, topo):
         tt(T.yc[:], ["yc"], T.y[:], T[dr][:], ["y", dr], OP.max)
         cp(T.yl[:], ["yl"], T.yc[:], ["yc"])
         ow = T[far][:, 0:WD]
-        act(T.Or[:], ["Or"], ow.indirect(T.yl[:]), [far, far + "d", "yl"], AF.Copy)
         act(T.XG[:], ["XG"], T.X[:, 0:WD].indirect(T.yl[:]), ["X", "Xd", "yl"], AF.Copy)
         cp(T.Yr[:], ["Yr"], T.IOTA[:, 0:WD].indirect(T.yl[:]), ["IOTA", "yl"])
         mm(T.pq[:, 0:256], ["pq"], T.IB[:], T.OFFB[:], ["IB", "OFFB"], True, False)
-        mm(T.pq[:, 0:256], ["pq"], T.IB[:], T.Or[:], ["IB", "Or"], False, False)
+        mm(T.ph[:, 0:256], ["ph"], T.I16[:], T.sm[:], ["I16", "sm"], True, False)
+        mm(T.ph[:, 0:256], ["ph"], T.IB[:], T.XG[:], ["IB", "XG"], False, True)
+        act(T.t2[:], ["t2"], T.ph[:, 0:256], ["ph"], AF.Copy, bias=8388608.0, scale=0.5)
+        act(T[xn][:], [xn], T.t2[:], ["t2"], AF.Copy, bias=-8388608.0)
+        act(T.Or[:], ["Or"], ow.indirect(T.yl[:]), [far, far + "d", "yl"], AF.Copy)
         base = 0
         for L in range(16):
             n = 256 - 16 * L
@@ -322,30 +382,27 @@ def rank_program(g, core, T, topo):
             ts(T.EQ[:, base:base + n], [e], T.Yr[:, 16 * L:256], ["Yr"], T.yc[:, L:L + 1], OP.is_equal, cols=["yc"])
             if n > 16:
                 mm(T.pq[:, 16 * L + 16:256], ["pq"], T.BO[:], T.EQ[:, base + 16:base + n], ["BO", e], False, False)
-            if L == 10:
-                mm(T.ph[:, 0:256], ["ph"], T.IB[:], T.XG[:], ["IB", "XG"], True, False)
-                mm(T.ph[:, 0:256], ["ph"], T.I16[:], T.sm[:], ["I16", "sm"], False, True)
+            if L == 15:
+                mm(T.pq[:, 0:256], ["pq"], T.IB8[:], T.Or[:], ["IB8", "Or"], False, False)
             mm(T.pq[:, 16 * L:16 * L + 16], ["pq"], T.TRI[:], T.EQ[:, base:base + 16], ["TRI", e], False, L == 15)
             base += n
-        act(T.t2[:], ["t2"], T.ph[:, 0:256], ["ph"], AF.Copy, bias=8388608.0, scale=0.5)
-        act(T[xn][:], [xn], T.t2[:], ["t2"], AF.Copy, bias=-8388608.0)
         tell = d < STEPS - 1
         dst = up if t == 0 else down
         if tell:
             send("X%d%d" % (t, d), dst, T["XI%d%d" % (t, d)][:], T[xn][:], [xn])
-        scan(T.qs[:], ["qs"], T.SEGB[:], T.pq[:, 0:256], ["SEGB", "pq"], 1.0e9, OP.max, OP.min)
-        ts(T.nw[:], ["nw"], T.qs[:, 15:256:16], ["qs"], 0.0, OP.is_ge, 8192.0, OP.mult)
-        tt(T.yw[:], ["yw"], T.yc[:], T.nw[:], ["yc", "nw"], OP.add)
-        tt(T.lf[:], ["lf"], T.yw[:], T.DC[:], ["yw", "DC"], OP.min)
+        scan(T.qs[:], ["qs"], T.SEGB[:], T.pq[:, 0:256], ["SEGB", "pq"], 1.0e10, OP.max, OP.min)
+        tt(T.nw[:], ["nw"], T.qs[:, 15:256:16], T.DC[:], ["qs", "DC"], OP.min)
+        tt(T.lf[:], ["lf"], T.yc[:], T.nw[:], ["yc", "nw"], OP.max)
         cp(T[l2][:], [l2], T.lf[:], ["lf"])
         if tell:
             send("L%d%d" % (t, d), dst, T["LI%d%d" % (t, d)][:], T[l2][:], [l2])
 
         def home():
-            tt(T.PLf[:], ["PLf"], T.PLf[:], T.yw[:], ["PLf", "yw"], OP.min)
+            tt(T.PLf[:], ["PLf"], T.PLf[:], T.lf[:], ["PLf", "lf"], OP.min)
             if d == STEPS - 1:
-                ts(T.lf[:], ["lf"], T.PLf[:], ["PLf"], float(WD), OP.min)
-                cp(T["PS%d" % t][:], ["PS%d" % t], T.lf[:], ["lf"])
+                ts(T.wd[:], ["wd"], T.PLf[:], ["PLf"], float(WN), OP.is_ge, 8192.0, OP.mult)
+                tt(T.wd[:], ["wd"], T.wd[:], T.PLf[:], ["wd", "PLf"], OP.max)
+                ts(T["PS%d" % t][:], ["PS%d" % t], T.wd[:], ["wd"], float(WD), OP.min)
                 fill(T.PLf[:], "PLf", 8192.0)
 
         def put_records():
@@ -355,26 +412,32 @@ def rank_program(g, core, T, topo):
             cp(ow.indirect(T[l2][:]), [far, far + "d"], T["vr%d" % t][:], ["vr%d" % t, l2])
 
         def small():
-            ts(T.wb[:], ["wb"], T.nw[:], ["nw"], 0.0, OP.is_equal)
-            mm(T.pt[:, 0:16], ["pt"], T.ONES[:], T.wb[:], ["ONES", "wb"], True, True)
             if tell:
-                tt(T.wd[:], ["wd"], T.wb[:], T.DC[:], ["wb", "DC"], OP.mult)
+                ts(T.TB[:], ["TB"], T.y[:], ["y"], -2048.0, OP.add)
+                mm(T.pc[0:16, 0:128], ["pc"], T.TB[:], T.I16[:], ["TB", "I16"], True, True)
+                tt(T.wd[:], ["wd"], T.DC[:], T.nw[:], ["DC", "nw"], OP.subtract)
+                cp(T.LT[0:16, :], ["LT"], T.pc[0:16, 0:128], ["pc"])
                 tt(T[dr][:], [dr], T[dr][:], T.wd[:], [dr, "wd"], OP.max)
-                ts(T.TB[:, 0:16], ["TB"], T.y[:], ["y"], -2048.0, OP.add)
-            op("v", g.vector.tensor_reduce, ["pt"], ["kf"], out=T.kf[:], in_=T.pt[:, 0:16], axis=AxisListType.X, op=OP.add)
-            cp(T.ki[:], ["ki"], T.kf[:], ["kf"])
-            ts(T.ka[:], ["ka"], T.ki[:], ["ki"], 31, OP.bitwise_and)
-            ts(T.TA[:, 32:33], ["TA"], T.ka[:], ["ka"], float(kd), OP.add)
 
-        return home, put_records, put_far, small
+        def kappa():
+            act(T.wb[:], ["wb"], T.qs[:, 15:256:16], ["qs"], AF.Relu, bias=1.0, scale=-1.0)
+            mm(T.pt[:, 0:1], ["pt"], T.ONE[:, 0:128], T.CK[:, 0:1], ["ONE", "CK"], True, False)
+            for L in range(16):
+                mm(T.pt[:, 0:1], ["pt"], T.ONE[:, 0:128], T.wb[:, L:L + 1], ["ONE", "wb"], False, L == 15)
+            act(T.k1[:], ["k1"], T.pt[:, 0:1], ["pt"], AF.Identity, bias=402653184.0)
+            act(T.kr[:], ["kr"], T.k1[:], ["k1"], AF.Copy, bias=402653184.0, scale=-1.0)
+            act(T.kf[:], ["kf"], T.pt[:, 0:1], ["pt", "kr"], AF.Identity, bias=T.kr[:])
+            act(T.KT[0:1, :], ["KT"], T.ONE[0:1, 0:128], ["ONE", "kf"], AF.Identity, bias=T.kf[0:1, :], scale=float(kd) + 15.5)
 
-    def next_z(t, d, far):
+        return home, put_records, put_far, small, kappa
+
+    def next_z(t, d):
         src = down if t == 0 else up
         xr = "XR%d" % t
         arrives("X%d%d" % (t, d), src, "XI%d%d" % (t, d))
         arrives("L%d%d" % (t, d), src, "LI%d%d" % (t, d))
         cp(T[xr][:, 0:WD].indirect(T["LI%d%d" % (t, d)][:]), [xr], T["XI%d%d" % (t, d)][:], [xr, "XI%d%d" % (t, d), "LI%d%d" % (t, d)])
-        cp(T.zb[:], ["zb"], T[xr][:, 0:WN].indirect(T.pl16[:]), [xr, "pl16"])
+        act(T.zb[:], ["zb"], T[xr][:, 0:WN].indirect(T.pl16[:]), [xr, "pl16"], AF.Copy)
 
     for t in range(2):
         far = "OB" if t == 0 else "OA"
@@ -388,34 +451,35 @@ def rank_program(g, core, T, topo):
                 hooks.append(lambda: near_update(0, "OA"))
             zn = "SR%d" % t if d == 0 else "zb"
             search(t, d, T[zn], zn, hooks)
-            home, put_records, put_far, small = pair(t, d, far, 97 * (d + 1) if d < STEPS - 1 else 0)
+            home, put_records, put_far, small, kappa = pair(t, d, far, 97 * (d + 1) if d < STEPS - 1 else 0)
             if d < STEPS - 1:
                 put_far()
                 tt(T.pm[:], ["pm"], T[far][:, 0:WD].indirect(T.yl[:]), T.DM[:], [far, far + "d", "yl", "DM"], OP.mult)
                 scan(T.ps[:], ["ps"], T.SEG[:], T.pm[:], ["SEG", "pm"], 0.0, OP.mult, OP.add)
                 cp(T.pl16[:], ["pl16"], T.ps[:, 15:256:16], ["ps"])
-                put_records()
-                home()
+                kappa()
                 small()
-                next_z(t, d, far)
+                home()
+                next_z(t, d)
+                put_records()
             elif t == 0:
                 put_records()
                 send_starts(1, down)
+                kappa()
                 put_far()
                 home()
                 send("P0", down, T.PR0[:], T.PS0[:], ["PS0"])
                 run_flags(1, "OB", down)
-                small()
                 arrives("S1", up, "SR1")
                 arrives("B1", up, "XR1")
                 arrives("D1", up, "DR1")
                 arrives("P0", up, "PR0")
             else:
+                put_records()
+                dma("y", "outx", [(T.yx[:], T.X[:, 0:WN])], ["X"], [])
                 home()
                 send("P1", up, T.PR1[:], T.PS1[:], ["PS1"])
                 arrives("P1", down, "PR1")
-                put_records()
-                dma("y", "outx", [(T.yx[:], T.X[:, 0:WN])], ["X"], [])
                 put_far()
                 dma("y", "outa", [(T.ya[:], T.OA[0:128:16, 0:WN])], ["OA"], [])
                 near_update(1, "OB")

from concourse.mybir import AluOpType as OP, AxisListType, ActivationFunctionType as AF

N = 5
WN = 4096
WD = 4352
STEPS = 3
NR = 4
SCH = [[(4, 8)], [(8, 12)], [(12, 16)], [(16, 20)], [(20, 24)], [(24, 28)], [(28, 30), (30, 32)]]
EARLY = 3
PORTIONS = ((0, 128, "pc", "pt"), (128, 512, "pla", "ph"))

SCRATCH = {}
for _n, _c, _d in (
        ("X", WD, "bfloat16"), ("XR0", WD, "bfloat16"), ("XR1", WD, "bfloat16"), ("OA", WD, "float32"), ("OB", WD, "float32"),
        ("IOTA", WD + 8, "float32"), ("A", 8192, "bfloat16"), ("M", 8192, "bfloat16"), ("zb", 256, "bfloat16"),
        ("pai", 256, "int32"), ("pbi", 256, "int32"), ("wti", 1, "int32"), ("wf", 1, "float32"), ("wg", 1, "float32"),
        ("pidx", 1, "int32"), ("pmi", 1, "int32"), ("pgi", 1, "int32"), ("pidf", 1, "float32"), ("pmf", 1, "float32"), ("pgf", 1, "float32"), ("pg15", 1, "float32"),
        ("kc", 8, "float32"),
        ("col", 256, "float32"), ("colL", 512, "float32"), ("colJ", 512, "float32"), ("colg", 128, "float32"), ("dl", 512, "float32"),
        ("E8", 144, "bfloat16"), ("E4n", 144, "bfloat16"), ("WG", 8, "float16"), ("GS", 8, "bfloat16"), ("CK", 2, "bfloat16"),
        ("I16", 128, "float16"), ("IB", 128, "bfloat16"), ("IB8", 128, "bfloat16"), ("INB", 128, "bfloat16"), ("IBAR", 128, "bfloat16"), ("BO", 128, "bfloat16"), ("TRI", 128, "bfloat16"), ("ONE", 512, "bfloat16"),
        ("DM", 256, "float32"), ("DMD", 256, "float32"), ("OFFB", 256, "bfloat16"), ("SEG", 256, "float32"), ("SEGB", 256, "float32"),
        ("RH", 512, "float16"), ("RU", 512, "float16"), ("RZ", 512, "float16"), ("RK", 512, "bfloat16"), ("RO", 512, "bfloat16"), ("KC", 128, "bfloat16"), ("KT", 128, "bfloat16"), ("vr0", 256, "float32"), ("vr1", 256, "float32"), ("DC", 16, "float32"),
        ("ui", 128, "int32"), ("u", 128, "int32"), ("sq", 128, "int32"), ("hm", 128, "int32"), ("UT", 128, "float16"), ("HT", 128, "float16"), ("ZT", 128, "float16"), ("LT", 128, "float16"), ("TB", 16, "float16"),
        ("RR", 512, "bfloat16"), ("LST", 512, "uint16"), ("c16", 512, "float16"), ("bar", 512, "bfloat16"),
        ("ym", 16, "float32"), ("yi", 16, "int32"), ("y", 16, "int32"), ("yc", 16, "float32"), ("yl", 16, "uint16"), ("Yr", 256, "uint16"), ("Or", 256, "bfloat16"),
        ("XG", 256, "bfloat16"), ("sm", 256, "float16"), ("t2", 256, "float32"), ("qs", 256, "float32"), ("nw", 16, "float32"), ("EQ", 2176, "bfloat16"),
        ("lf", 16, "float32"), ("pm", 256, "float32"), ("ps", 256, "float32"), ("pl16", 16, "uint16"), ("PLf", 16, "float32"), ("wb", 16, "bfloat16"), ("wd", 16, "float32"),
        ("k1", 1, "float32"), ("kr", 1, "float32"), ("kf", 1, "float32")):
    SCRATCH[_n] = ("sbuf", [128, _c], _d)
for _t in range(2):
    for _n, _c, _d in (("SS", 256, "bfloat16"), ("SR", 256, "bfloat16"), ("DS", 16, "float32"), ("DR", 16, "float32"), ("PS", 16, "uint16"), ("PR", 16, "uint16")):
        SCRATCH["%s%d" % (_n, _t)] = ("sbuf", [128, _c], _d)
    for _s in range(STEPS):
        SCRATCH["XN%d" % _s] = ("sbuf", [128, 256], "bfloat16")
        SCRATCH["L2%d" % _s] = ("sbuf", [128, 16], "uint16")
        if _s < STEPS - 1:
            SCRATCH["XI%d%d" % (_t, _s)] = ("sbuf", [128, 256], "bfloat16")
            SCRATCH["LI%d%d" % (_t, _s)] = ("sbuf", [128, 16], "uint16")
SCRATCH["oad"] = ("dram", [8, WN], "float32")
SCRATCH["obd"] = ("dram", [8, WN], "float32")
for _n, _c in (("pz", 1024), ("ph", 512), ("pt", 512), ("pc", 512), ("pla", 512), ("pk", 512), ("pq", 512)):
    SCRATCH[_n] = ("psum", [128, _c], "float32")
PARTS = ("ym", "RO", "RZ", "A0")
PSUM = ("pz", "ph", "pt", "pc", "pla", "pk", "pq")

MSG = []
for _t in range(2):
    MSG += ["S%d" % _t, "B%d" % _t, "D%d" % _t, "P%d" % _t]
    for _s in range(STEPS - 1):
        MSG += ["X%d%d" % (_t, _s), "L%d%d" % (_t, _s)]
SEMAPHORES = ["cv", "cs", "cp", "cg", "ldx", "ldw", "lda", "ldb", "sta", "stb", "roa", "rob", "outx", "outa", "outb"]
SEMAPHORES += ["a" + m for m in MSG] + ["d" + m for m in MSG]


def rank_program(g, core, T, topo):
    me = T.rank_of(core)
    if me is None:
        return
    queues = {"v": g.vector, "s": g.scalar, "p": g.tensor, "g": g, "y": g.sync}
    csem = {"v": "cv", "s": "cs", "p": "cp", "g": "cg"}
    count, waited, wr, rd = {}, {q: {} for q in queues}, {}, {}

    def wait(q, toks):
        for _, sem, val in toks:
            if waited[q].get(sem, 0) < val:
                waited[q][sem] = val
                queues[q].wait_ge(T.sem[sem], val)

    def before(q, reads, writes):
        toks = []
        for x in reads:
            toks += wr.get(x, [])
            if x in PSUM:
                toks += [k for k in rd.get(x, []) if k[0] != q]
        for x in writes:
            toks += [k for k in wr.get(x, []) if k[0] != q or (q != "p" and x not in PARTS)]
            toks += [k for k in rd.get(x, []) if k[0] != q]
        best = {}
        for k in toks:
            if k[1] not in best or best[k[1]][2] < k[2]:
                best[k[1]] = k
        wait(q, best.values())

    def after(tok, reads, writes):
        for x in reads:
            if x not in writes:
                rd.setdefault(x, [])
                rd[x] = [k for k in rd[x] if k[1] != tok[1]] + [tok]
        for x in writes:
            wr[x] = [tok]
            rd[x] = []

    def op(q, fn, reads, writes, **kw):
        before(q, reads, writes)
        sem = csem[q]
        fn(**kw).then_inc(T.sem[sem], 1)
        count[sem] = count.get(sem, 0) + 1
        after((q, sem, count[sem]), reads, writes)

    def dma(q, sem, pairs, reads, writes):
        before(q, reads, writes)
        for out, in_ in pairs:
            queues[q].dma_start(out, in_).then_inc(T.sem[sem], 16)
            count[sem] = count.get(sem, 0) + 16
        after(("dma" + sem, sem, count[sem]), reads, writes)

    def send(msg, dst, out, in_, reads):
        before("g", reads, [])
        eng = topo.engines(core, dst)[:8]
        rid, pid, _ = topo.addr(dst)
        g.remote_dma(out, in_, T.sem["a" + msg], T.sem["d" + msg], pid, rid, sum(1 << e for e in eng))
        count["d" + msg] = len(eng)
        after(("rdma" + msg, "d" + msg, len(eng)), reads, [])

    def arrives(msg, src, buf):
        n = len(topo.engines(src, core)[:8])
        count["a" + msg] = n
        after(("arr" + msg, "a" + msg, n), [], [buf])

    def ts(out, w, in0, r, s1, op0, s2=None, op1=None, cols=()):
        kw = {"out": out, "in0": in0, "scalar1": s1, "scalar2": s2, "op0": op0}
        if op1 is not None:
            kw["op1"] = op1
        op("v", g.vector.tensor_scalar, list(r) + list(cols), w, **kw)

    def tt(out, w, in0, in1, r, o):
        op("v", g.vector.tensor_tensor, r, w, out=out, in0=in0, in1=in1, op=o)

    def cp(out, w, in_, r):
        op("v", g.vector.tensor_copy, r, w, out=out, in_=in_)

    def mm(out, w, lhsT, rhs, r, start, stop):
        op("p", g.tensor.matmul, r, w, out=out, lhsT=lhsT, rhs=rhs, start=start, stop=stop)

    def act(out, w, in_, r, func, **kw):
        op("s", g.scalar.activation, r, w, out=out, in_=in_, func=func, **kw)

    def scan(out, w, d0, d1, r, init, o0, o1):
        op("v", g.vector.tensor_tensor_scan, r, w, out=out, data0=d0, data1=d1, initial=init, op0=o0, op1=o1)

    up, down = T.cores[(me + 1) % N], T.cores[(me - 1) % N]

    dma("s", "ldx", [(T.X[:, 0:WN], T.x[:])], [], ["X"])
    dma("y", "ldw", [(T.wti[:], T.wt[:])], [], ["wti"])
    dma("y", "lda", [(T.pai[:], T.pa[:])], [], ["pai"])
    dma("y", "ldb", [(T.pbi[:], T.pb[:])], [], ["pbi"])

    def iota(name, pattern, base, mult, n):
        kw = {"out": T[name][:, 0:n], "pattern": pattern, "base": base, "channel_multiplier": mult}
        if name != "pidx":
            kw["allow_small_or_imprecise_dtypes"] = True
        op("g", g.iota, [], [name], **kw)

    iota("pidx", [[0, 1]], 0, 1, 1)
    iota("col", [[1, 256]], 0, 0, 256)
    iota("colL", [[0, 32], [1, 16]], 0, 0, 512)
    iota("colg", [[1, 8], [0, 16]], 0, 0, 128)
    iota("colJ", [[2, 32], [0, 16]], 1, 0, 512)

    def send_starts(t, dst):
        act(T["SS%d" % t][:], ["SS%d" % t], T.X[:, t:WN:16], ["X"], AF.Copy)
        send("S%d" % t, dst, T["SR%d" % t][:], T["SS%d" % t][:], ["SS%d" % t])
        send("B%d" % t, dst, T["XR%d" % t][:, 0:WN], T.X[:, 0:WN], ["X"])

    send_starts(0, up)
    arrives("S0", down, "SR0")
    arrives("B0", down, "XR0")
    iota("IOTA", [[1, WD]], 0, 0, WD)

    def fill(ap, w, c):
        before("v", [], [w])
        g.vector.memset(ap, c).then_inc(T.sem.cv, 1)
        count["cv"] = count.get("cv", 0) + 1
        after(("v", "cv", count["cv"]), [], [w])

    fill(T.X[:, WN:WD], "Xd", 0.0)
    fill(T.OA[:, WN:WD], "OAd", 0.0)
    fill(T.OB[:, WN:WD], "OBd", 0.0)
    fill(T.IOTA[:, WD:WD + 8], "IOTAd", -1.0)
    fill(T.ONE[:], "ONE", 1.0)
    fill(T.KT[:], "KT", 0.0)
    fill(T.CK[:], "CK", -15.5 / 128)
    fill(T.PLf[:], "PLf", 8192.0)
    ts(T.pmi[:], ["pmi"], T.pidx[:], ["pidx"], 15, OP.bitwise_and)
    ts(T.pgi[:], ["pgi"], T.pidx[:], ["pidx"], 4, OP.arith_shift_right)
    cp(T.pidf[:], ["pidf"], T.pidx[:], ["pidx"])
    cp(T.pmf[:], ["pmf"], T.pmi[:], ["pmi"])
    cp(T.pgf[:], ["pgf"], T.pgi[:], ["pgi"])
    ts(T.pg15[:], ["pg15"], T.pgf[:], ["pgf"], 16.0, OP.mult, 15.0, OP.add)
    for nm, val in (("E8", 8192.0), ("E4n", -4096.0)):
        ts(T[nm][:], [nm], T.col[:, 0:144], ["col"], T.pg15[:], OP.is_equal, val, OP.mult, cols=["pg15"])
    ts(T.GS[:], ["GS"], T.col[:, 0:8], ["col"], T.pgf[:], OP.is_equal, cols=["pgf"])
    for nm, val in (("I16", 1.0), ("IB", 1.0), ("INB", -1.0), ("IBAR", 16777216.0)):
        ts(T[nm][:], [nm], T.col[:, 0:128], ["col"], T.pidf[:], OP.is_equal, val, OP.mult, cols=["pidf"])
    ts(T.dl[:], ["dl"], T.colL[:], ["colL"], T.pmf[:], OP.is_equal, cols=["pmf"])
    cp(T.RH[:], ["RH"], T.dl[:], ["dl"])
    tt(T.RU[:], ["RU"], T.colJ[:], T.dl[:], ["colJ", "dl"], OP.mult)
    h0, g1, g3, e1, r1, r2, kv, rv = [T.kc[:, i:i + 1] for i in range(8)]
    ts(h0, ["h0"], T.pidf[:], ["pidf"], 0.0, OP.is_equal, 0.5, OP.mult)
    ts(g1, ["g1"], T.pidf[:], ["pidf"], 1.0, OP.is_ge, 2048.0, OP.mult)
    ts(g3, ["g3"], T.pidf[:], ["pidf"], 3.0, OP.is_ge, -8.0, OP.mult)
    ts(e1, ["e1"], T.pidf[:], ["pidf"], 1.0, OP.is_equal, -1.0, OP.mult)
    ts(r1, ["r1"], T.pidf[:], ["pidf"], 1.0, OP.is_ge, -4096.0, OP.mult)
    ts(r2, ["r2"], T.pidf[:], ["pidf"], 2.0, OP.is_ge, -4096.0, OP.mult)
    tt(kv, ["kv"], h0, g1, ["h0", "g1"], OP.add)
    ts(rv, ["rv"], T.pidf[:], ["pidf"], 0.0, OP.is_equal, e1, OP.add, cols=["e1"])
    tt(kv, ["kv"], kv, g3, ["kv", "g3"], OP.add)
    ts(T.RK[:], ["RK"], T.ONE[:], ["ONE"], rv, OP.mult, cols=["rv"])
    ts(T.KC[:], ["KC"], T.ONE[:, 0:128], ["ONE"], kv, OP.mult, cols=["kv"])
    cp(T.wf[:], ["wf"], T.wti[:], ["wti"])
    ts(T.wg[:], ["wg"], T.wf[:], ["wf"], 2048.0, OP.is_gt, -4096.0, OP.mult)
    tt(T.wg[:], ["wg"], T.wg[:], T.wf[:], ["wg", "wf"], OP.add)
    ts(T.WG[:], ["WG"], T.GS[:], ["GS"], T.wg[:], OP.mult, cols=["wg"])
    c0 = 16 * NR
    ts(T.RO[:, c0:512], ["RO"], T.ONE[:, c0:512], ["ONE"], r1, OP.mult, cols=["r1"])
    ts(T.RO[:, 0:c0], ["RO"], T.ONE[:, 0:c0], ["ONE"], r2, OP.mult, cols=["r2"])
    ts(T.RZ[:, c0:512], ["RZ"], T.RH[:, c0:512], ["RH"], -4096.0, OP.mult)
    ts(T.RZ[:, 0:c0], ["RZ"], T.RH[:, 0:c0], ["RH"], 0.0, OP.mult)
    cp(T.qs[:], ["qs"], T.pai[:], ["pai"])
    cp(T.t2[:], ["t2"], T.pbi[:], ["pbi"])
    dma("y", "sta", [(T.oad[:], T.qs[:])], ["qs"], ["oad"])
    dma("y", "stb", [(T.obd[:], T.t2[:])], ["t2"], ["obd"])
    dma("y", "roa", [(T.OA[m::16, 0:WN], T.oad[:]) for m in range(16)], ["oad"], ["OA"])
    dma("y", "rob", [(T.OB[m::16, 0:WN], T.obd[:]) for m in range(16)], ["obd"], ["OB"])

    def late_constants():
        ts(T.IB8[:], ["IB8"], T.IB[:], ["IB"], 8192.0, OP.mult)
        ts(T.BO[:], ["BO"], T.colg[:], ["colg"], T.pgf[:], OP.is_equal, 8192.0, OP.mult, cols=["pgf"])
        ts(T.TRI[:], ["TRI"], T.colL[:, 0:128], ["colL"], T.pmf[:], OP.is_gt, cols=["pmf"])
        tt(T.TRI[:], ["TRI"], T.TRI[:], T.BO[:], ["TRI", "BO"], OP.mult)
        ts(T.DM[:], ["DM"], T.colL[:, 0:256], ["colL"], T.pmf[:], OP.is_equal, cols=["pmf"])
        ts(T.OFFB[:], ["OFFB"], T.colL[:, 0:256], ["colL"], T.pmf[:], OP.not_equal, 1073741824.0, OP.mult, cols=["pmf"])
        ts(T.OFFB[:], ["OFFB"], T.OFFB[:], ["OFFB"], 8192.0, OP.add)
        ts(T.SEG[:], ["SEG"], T.colL[:, 0:256], ["colL"], 0.0, OP.not_equal)
        ts(T.SEGB[:], ["SEGB"], T.colL[:, 0:256], ["colL"], 0.0, OP.is_equal, 2.0e10, OP.mult)
        ts(T.SEGB[:], ["SEGB"], T.SEGB[:], ["SEGB"], -1.0e10, OP.add)
        ts(T.DMD[:], ["DMD"], T.col[:], ["col"], 4097.0, OP.add)
        tt(T.DMD[:], ["DMD"], T.DMD[:], T.DM[:], ["DMD", "DM"], OP.mult)
        ts(T.vr0[:], ["vr0"], T.col[:], ["col"], 16.0, OP.mult)
        ts(T.vr1[:], ["vr1"], T.col[:], ["col"], 16.0, OP.mult, 1.0, OP.add)
        ts(T.DC[:], ["DC"], T.col[:, 0:16], ["col"], 16.0, OP.mult, T.pmf[:], OP.add, cols=["pmf"])
        ts(T.DC[:], ["DC"], T.DC[:], ["DC"], 4096.0, OP.add)

    late_constants()

    def run_flags(t, near, dst):
        ts(T.pm[:], ["pm"], T[near][:, t:WN:16], [near], 0.0, OP.is_ge)
        tt(T.pm[:], ["pm"], T.pm[:], T.DMD[:], ["pm", "DMD"], OP.mult)
        scan(T.ps[:], ["ps"], T.SEG[:], T.pm[:], ["SEG", "pm"], 0.0, OP.mult, OP.add)
        ts(T["DS%d" % t][:], ["DS%d" % t], T.ps[:, 15:256:16], ["ps"], -1.0, OP.add)
        send("D%d" % t, dst, T["DR%d" % t][:], T["DS%d" % t][:], ["DS%d" % t])

    def near_update(t, near):
        tab = T[near][:, t:WN:16]
        tt(tab, [near], T.IOTA[:, 0:WD + 8].indirect(T["PR%d" % t][:]), tab, ["IOTA", "IOTAd", "PR%d" % t, near], OP.max)

    def search(t, d, z, zr, hooks):
        for l in range(16):
            mm(T.ph[0:16, l:128:16], ["ph"], z[:, l:256:16], T.WG[:], ["WG", zr], True, True)
        for l in range(16):
            mm(T.pq[0:16, l:128:16], ["pq"], z[:, l:256:16], T.GS[:], ["GS", zr], True, True)

        def raw1(a, b, bank):
            mm(T[bank][:, a:b], [bank], T.KC[0:4, :], T.RK[0:4, a:b], ["KC", "RK"], True, False)
            mm(T[bank][:, a:b], [bank], T.KT[0:1, :], T.ONE[0:1, a:b], ["KT", "ONE"], False, False)

        def raw2(a, b, bank):
            mm(T[bank][:, a:b], [bank], T.UT[0:16, :], T.RU[0:16, a:b], ["UT", "RU"], False, False)

        def raw3(a, b, bank, stop):
            mm(T[bank][:, a:b], [bank], T.HT[0:16, :], T.RH[0:16, a:b], ["HT", "RH"], False, stop)

        (a0, b0, s0, e0), (a1, b1, s1, e1) = PORTIONS
        raw1(a0, b0, s0)
        raw1(a1, b1, s1)
        raw1(a0, b0, e0)
        cp(T.ui[0:16, :], ["ui"], T.ph[0:16, 0:128], ["ph"])
        ts(T.u[0:16, :], ["u"], T.ui[0:16, :], ["ui"], 4095, OP.bitwise_and)
        tt(T.sq[0:16, :], ["sq"], T.u[0:16, :], T.u[0:16, :], ["u"], OP.mult)
        ts(T.UT[0:16, :], ["UT"], T.u[0:16, :], ["u"], -2048.0, OP.add)
        ts(T.hm[0:16, :], ["hm"], T.sq[0:16, :], ["sq"], 5, OP.arith_shift_right, 4095, OP.bitwise_and)
        ts(T.HT[0:16, :], ["HT"], T.hm[0:16, :], ["hm"], -2048.0, OP.add)
        raw2(a0, b0, s0)
        raw2(a1, b1, s1)
        raw2(a0, b0, e0)
        raw3(a0, b0, s0, True)
        raw3(a0, b0, e0, False)
        raw3(a1, b1, s1, True)

        def near(i):
            a, b, bank, rest = PORTIONS[i]
            ts(T.RR[:, a:b], ["RR%d" % i], T[bank][:, a:b], [bank], 51539607552.0, OP.add, -51539607552.0, OP.add)
            mm(T[rest][:, a:b], [rest], T.INB[:], T.RR[:, a:b], ["INB", "RR%d" % i], False, True)

        def lists(i):
            a, b, _, rest = PORTIONS[i]
            ts(T.LST[:, a:b], ["LST%d" % i], T[rest][:, a:b], [rest], 2047.5, OP.add)

        near(0)
        raw1(a1, b1, e1)
        raw2(a1, b1, e1)
        raw3(a1, b1, e1, False)
        ts(T.ZT[0:16, :], ["ZT"], T.pq[0:16, 0:128], ["pq"], -2048.0, OP.add)
        for i in range(4):
            mm(T.pz[:, 256 * i:256 * i + 256], ["pz"], T.IB[:], z[:], ["IB", zr], True, True)
        lists(0)
        near(1)
        win = T.X[:, 0:WN]
        for pieces in SCH:
            for j0, j1 in pieces:
                if 16 * j1 <= PORTIONS[0][1]:
                    act(T.A[:, 256 * j0:256 * j1], ["A%d" % j0], win.indirect(T.LST[:, 16 * j0:16 * j1]), ["X", "LST0"], AF.Copy)
        mm(T.pk[:], ["pk"], T.KC[0:4, :], T.RO[0:4, :], ["KC", "RO"], True, False)
        mm(T.pk[:], ["pk"], T.ZT[0:16, :], T.RZ[0:16, :], ["ZT", "RZ"], False, False)
        if d > 0:
            mm(T.pc[:], ["pc"], T.LT[0:16, :], T.RH[0:16, :], ["LT", "RH"], True, True)

        def sums(src, sel, pieces):
            j0, j1 = pieces[0][0], pieces[-1][1]
            for l in range(16):
                mm(T.pk[:, 16 * j0:16 * j1], ["pk"], T[sel][:, 15 - l:143 - l], T[src][:, 256 * j0 + l:256 * j1:16], [sel] + ["%s%d" % (src, a) for a, _ in pieces], False, False)

        if NR:
            for j in range(NR):
                if j == NR // 2:
                    lists(1)
                    for pieces in SCH:
                        for j0, j1 in pieces:
                            if 16 * j1 > PORTIONS[0][1]:
                                act(T.A[:, 256 * j0:256 * j1], ["A%d" % j0], win.indirect(T.LST[:, 16 * j0:16 * j1]), ["X", "LST1"], AF.Copy)
                tt(T.A[:, 256 * j:256 * j + 256], ["A0"], win.indirect(T.LST[:, 16 * j:16 * j + 16]), z[:], ["X", "LST0", zr], OP.subtract)
            ts(T.M[:, 0:256 * NR], ["M0"], T.A[:, 0:256 * NR], ["A0"], 0.0, OP.max)
        sums("A", "E4n", SCH[0])
        if NR:
            sums("A", "E4n", [(0, NR)])
            sums("M", "E8", [(0, NR)])
        ts(T.c16[:], ["c16"], T.LST[:], ["LST0", "LST1"], -2048.0, OP.add)
        if d > 0:
            tt(T.bar[:], ["bar"], T.c16[:], T.pc[:], ["c16", "pc"], OP.is_equal)
        else:
            ts(T.sm[:], ["sm"], z[:], [zr], -0.5, OP.add)
        for k, pieces in enumerate(SCH):
            for j0, j1 in pieces:
                tt(T.M[:, 256 * j0:256 * j1], ["M%d" % j0], T.A[:, 256 * j0:256 * j1], T.pz[:, 0:256 * (j1 - j0)], ["A%d" % j0, "pz"], OP.max)
            if k == 0 and d > 0:
                mm(T.pk[:], ["pk"], T.IBAR[:], T.bar[:], ["IBAR", "bar"], False, False)
            if k < EARLY:
                sums("A", "E4n", SCH[k + 1])
            sums("M", "E8", pieces)
            if k == len(SCH) - 2:
                mm(T.pk[:, 0:16 * SCH[-1][0][0]], ["pk"], T.I16[:], T.c16[:, 0:16 * SCH[-1][0][0]], ["I16", "c16"], False, False)
            if EARLY <= k < len(SCH) - 1:
                sums("A", "E4n", SCH[k + 1])
            if k == 4:
                for h in hooks:
                    h()
        mm(T.pk[:, 16 * SCH[-1][0][0]:512], ["pk"], T.I16[:], T.c16[:, 16 * SCH[-1][0][0]:512], ["I16", "c16"], False, True)
        for L in range(16):
            op("v", g.vector.tensor_reduce, ["pk"], ["ym"], out=T.ym[:, L:L + 1], in_=T.pk[:, L:512:16], axis=AxisListType.X, op=OP.min)

    def pair(t, d, far, kd):
        xn, l2 = "XN%d" % d, "L2%d" % d
        dr = "DR%d" % t
        ts(T.yi[:], ["yi"], T.ym[:], ["ym"], 2048.0, OP.add)
        ts(T.y[:], ["y"], T.yi[:], ["yi"], 4095, OP.bitwise_and)
        tt(T.yc[:], ["yc"], T.y[:], T[dr][:], ["y", dr], OP.max)
        cp(T.yl[:], ["yl"], T.yc[:], ["yc"])
        ow = T[far][:, 0:WD]
        act(T.XG[:], ["XG"], T.X[:, 0:WD].indirect(T.yl[:]), ["X", "Xd", "yl"], AF.Copy)
        cp(T.Yr[:], ["Yr"], T.IOTA[:, 0:WD].indirect(T.yl[:]), ["IOTA", "yl"])
        mm(T.pq[:, 0:256], ["pq"], T.IB[:], T.OFFB[:], ["IB", "OFFB"], True, False)
        mm(T.ph[:, 0:256], ["ph"], T.I16[:], T.sm[:], ["I16", "sm"], True, False)
        mm(T.ph[:, 0:256], ["ph"], T.IB[:], T.XG[:], ["IB", "XG"], False, True)
        act(T.t2[:], ["t2"], T.ph[:, 0:256], ["ph"], AF.Copy, bias=8388608.0, scale=0.5)
        act(T[xn][:], [xn], T.t2[:], ["t2"], AF.Copy, bias=-8388608.0)
        act(T.Or[:], ["Or"], ow.indirect(T.yl[:]), [far, far + "d", "yl"], AF.Copy)
        base = 0
        for L in range(16):
            n = 256 - 16 * L
            e = "EQ%d" % L
            ts(T.EQ[:, base:base + n], [e], T.Yr[:, 16 * L:256], ["Yr"], T.yc[:, L:L + 1], OP.is_equal, cols=["yc"])
            if n > 16:
                mm(T.pq[:, 16 * L + 16:256], ["pq"], T.BO[:], T.EQ[:, base + 16:base + n], ["BO", e], False, False)
            if L == 15:
                mm(T.pq[:, 0:256], ["pq"], T.IB8[:], T.Or[:], ["IB8", "Or"], False, False)
            mm(T.pq[:, 16 * L:16 * L + 16], ["pq"], T.TRI[:], T.EQ[:, base:base + 16], ["TRI", e], False, L == 15)
            base += n
        tell = d < STEPS - 1
        dst = up if t == 0 else down
        if tell:
            send("X%d%d" % (t, d), dst, T["XI%d%d" % (t, d)][:], T[xn][:], [xn])
        scan(T.qs[:], ["qs"], T.SEGB[:], T.pq[:, 0:256], ["SEGB", "pq"], 1.0e10, OP.max, OP.min)
        tt(T.nw[:], ["nw"], T.qs[:, 15:256:16], T.DC[:], ["qs", "DC"], OP.min)
        tt(T.lf[:], ["lf"], T.yc[:], T.nw[:], ["yc", "nw"], OP.max)
        cp(T[l2][:], [l2], T.lf[:], ["lf"])
        if tell:
            send("L%d%d" % (t, d), dst, T["LI%d%d" % (t, d)][:], T[l2][:], [l2])

        def home():
            tt(T.PLf[:], ["PLf"], T.PLf[:], T.lf[:], ["PLf", "lf"], OP.min)
            if d == STEPS - 1:
                ts(T.wd[:], ["wd"], T.PLf[:], ["PLf"], float(WN), OP.is_ge, 8192.0, OP.mult)
                tt(T.wd[:], ["wd"], T.wd[:], T.PLf[:], ["wd", "PLf"], OP.max)
                ts(T["PS%d" % t][:], ["PS%d" % t], T.wd[:], ["wd"], float(WD), OP.min)
                fill(T.PLf[:], "PLf", 8192.0)

        def put_records():
            cp(T.X[:, 0:WD].indirect(T[l2][:]), ["X", "Xd"], T[xn][:], [xn, l2])

        def put_far():
            cp(ow.indirect(T[l2][:]), [far, far + "d"], T["vr%d" % t][:], ["vr%d" % t, l2])

        def small():
            if tell:
                ts(T.TB[:], ["TB"], T.y[:], ["y"], -2048.0, OP.add)
                mm(T.pc[0:16, 0:128], ["pc"], T.TB[:], T.I16[:], ["TB", "I16"], True, True)
                tt(T.wd[:], ["wd"], T.DC[:], T.nw[:], ["DC", "nw"], OP.subtract)
                cp(T.LT[0:16, :], ["LT"], T.pc[0:16, 0:128], ["pc"])
                tt(T[dr][:], [dr], T[dr][:], T.wd[:], [dr, "wd"], OP.max)

        def kappa():
            act(T.wb[:], ["wb"], T.qs[:, 15:256:16], ["qs"], AF.Relu, bias=1.0, scale=-1.0)
            mm(T.pt[:, 0:1], ["pt"], T.ONE[:, 0:128], T.CK[:, 0:1], ["ONE", "CK"], True, False)
            for L in range(16):
                mm(T.pt[:, 0:1], ["pt"], T.ONE[:, 0:128], T.wb[:, L:L + 1], ["ONE", "wb"], False, L == 15)
            act(T.k1[:], ["k1"], T.pt[:, 0:1], ["pt"], AF.Identity, bias=402653184.0)
            act(T.kr[:], ["kr"], T.k1[:], ["k1"], AF.Copy, bias=402653184.0, scale=-1.0)
            act(T.kf[:], ["kf"], T.pt[:, 0:1], ["pt", "kr"], AF.Identity, bias=T.kr[:])
            act(T.KT[0:1, :], ["KT"], T.ONE[0:1, 0:128], ["ONE", "kf"], AF.Identity, bias=T.kf[0:1, :], scale=float(kd) + 15.5)

        return home, put_records, put_far, small, kappa

    def next_z(t, d):
        src = down if t == 0 else up
        xr = "XR%d" % t
        arrives("X%d%d" % (t, d), src, "XI%d%d" % (t, d))
        arrives("L%d%d" % (t, d), src, "LI%d%d" % (t, d))
        cp(T[xr][:, 0:WD].indirect(T["LI%d%d" % (t, d)][:]), [xr], T["XI%d%d" % (t, d)][:], [xr, "XI%d%d" % (t, d), "LI%d%d" % (t, d)])
        act(T.zb[:], ["zb"], T[xr][:, 0:WN].indirect(T.pl16[:]), [xr, "pl16"], AF.Copy)

    for t in range(2):
        far = "OB" if t == 0 else "OA"
        near = "OA" if t == 0 else "OB"
        for d in range(STEPS):
            hooks = []
            if (t, d) == (0, 0):
                hooks.append(lambda: run_flags(0, "OA", up))
                hooks.append(lambda: arrives("D0", down, "DR0"))
            if (t, d) == (1, 0):
                hooks.append(lambda: near_update(0, "OA"))
            zn = "SR%d" % t if d == 0 else "zb"
            search(t, d, T[zn], zn, hooks)
            home, put_records, put_far, small, kappa = pair(t, d, far, 97 * (d + 1) if d < STEPS - 1 else 0)
            if d < STEPS - 1:
                put_far()
                tt(T.pm[:], ["pm"], T[far][:, 0:WD].indirect(T.yl[:]), T.DM[:], [far, far + "d", "yl", "DM"], OP.mult)
                scan(T.ps[:], ["ps"], T.SEG[:], T.pm[:], ["SEG", "pm"], 0.0, OP.mult, OP.add)
                cp(T.pl16[:], ["pl16"], T.ps[:, 15:256:16], ["ps"])
                kappa()
                small()
                home()
                next_z(t, d)
                put_records()
            elif t == 0:
                put_records()
                send_starts(1, down)
                kappa()
                put_far()
                home()
                send("P0", down, T.PR0[:], T.PS0[:], ["PS0"])
                run_flags(1, "OB", down)
                arrives("S1", up, "SR1")
                arrives("B1", up, "XR1")
                arrives("D1", up, "DR1")
                arrives("P0", up, "PR0")
            else:
                put_records()
                dma("y", "outx", [(T.yx[:], T.X[:, 0:WN])], ["X"], [])
                home()
                send("P1", up, T.PR1[:], T.PS1[:], ["PS1"])
                arrives("P1", down, "PR1")
                put_far()
                dma("y", "outa", [(T.ya[:], T.OA[0:128:16, 0:WN])], ["OA"], [])
                near_update(1, "OB")
                dma("y", "outb", [(T.yb[:], T.OB[0:128:16, 0:WN])], ["OB"], [])
    for sem in sorted(count):
        wait("g", [("", sem, count[sem])])
